import numpy as np
import ml_dtypes


def mxq(x, axis, fmt="e4m3"):
    dtype, down = {"e4m3": (ml_dtypes.float8_e4m3fn, 7), "e5m2": (ml_dtypes.float8_e5m2, 14)}[fmt]
    v = np.moveaxis(np.asarray(x, np.float32).astype(ml_dtypes.bfloat16).astype(np.float64), axis, -1)
    blocks = v.reshape(v.shape[:-1] + (-1, 32))
    amax = np.abs(blocks).max(-1, keepdims=True)
    byte = np.maximum(np.where(amax > 0, np.frexp(amax)[1] - 1 + 127, 0) - down, 1)
    scale = np.exp2(byte - 127.0)
    codes = (blocks / scale).astype(np.float32).astype(dtype).astype(np.float64)
    return np.moveaxis((codes * scale).reshape(v.shape), -1, axis)


WIDE = False


def mx_kscale(k):
    if not WIDE:
        return np.ones(k)
    levels = np.array([10, -10, 5, -5, 0])
    if k % 512:
        return np.exp2(np.random.permutation(np.resize(levels, k // 32))).repeat(32)
    a = np.empty((k // 512, 16))
    for p in range(k // 512):
        a[p, :8] = np.random.permutation(np.resize(levels, 8))
        for g in range(8):
            far = levels[np.abs(levels - a[p, g]) >= 10]
            a[p, g + 8] = far[np.random.randint(len(far))]
    return np.exp2(a.ravel()).repeat(32)


BF16 = ml_dtypes.bfloat16


def bf(x):
    return np.asarray(x, np.float32).astype(BF16)


def f64(x):
    return np.asarray(x).astype(np.float64)

def planes(Y):
    n, m = Y.shape
    b = f64(bf(Y)).reshape(n // 32, 32, m)
    amax = np.abs(b).max(1)
    byte = np.clip(np.where(amax > 0, np.frexp(amax)[1] - 1 + 127 - 7, 1), 1, 254)
    codes = (b * np.exp2(127.0 - byte)[:, None, :]).reshape(n, m).astype(np.float32).astype(ml_dtypes.float8_e4m3fn).view(np.uint8)
    words = codes.reshape(n // 512, 128, 4, m).transpose(0, 1, 3, 2)
    return np.ascontiguousarray(words), np.ascontiguousarray(byte.astype(np.uint8).reshape(n // 512, 16, m))


B, GH, GW, T, K, D = 2, 16, 32, 1024, 3072, 1024


def setup_inputs():
    s = mx_kscale(K)
    contrast = np.exp(0.8 * np.random.randn(T, 1))
    patches = contrast * np.random.randn(T, K)
    w_embed = np.random.randn(K, D) / np.sqrt(K)
    return {
        "patches": bf(patches * s[None, :]),
        "w_embed": bf(w_embed / s[:, None]),
        "bias": bf(0.3 * np.random.randn(D)),
        "row_pos": bf(0.4 * np.random.randn(GH, D)),
        "col_pos": bf(0.4 * np.random.randn(GW, D)),
    }


def reference(patches, w_embed, bias, row_pos, col_pos):
    xq = mxq(f64(patches), 1, "e4m3")
    wq = mxq(f64(w_embed), 0, "e4m3")
    e = xq @ wq
    grid = e.reshape(B, GH, GW, D) + f64(bias)
    grid = grid + f64(row_pos)[None, :, None, :]
    grid = grid + f64(col_pos)[None, None, :, :]
    y = grid.reshape(T, D)
    Y = y.reshape(T, D)
    words, scales = planes(Y)
    return y, words, scales

@@ -1,0 +1,299 @@
+from contextlib import ExitStack
+
+import concourse.mybir as mybir
+from concourse.masks import make_identity
+
+GH, GW, T, K, D = 16, 32, 1024, 3072, 1024
+FLOPS = 2 * T * K * D
+
+F32 = mybir.dt.float32
+BF16 = mybir.dt.bfloat16
+I32 = mybir.dt.int32
+U32 = mybir.dt.uint32
+U8 = mybir.dt.uint8
+FP8X4 = mybir.dt.float8_e4m3fn_x4
+ADD = mybir.AluOpType.add
+
+P = 128
+PACK = 4
+SPAN = P * PACK
+PASSES = K // SPAN
+CHUNKS = 2 * PASSES
+RAW_BUFS = 8
+W_VECTOR_COLS_FIRST = 320
+W_VECTOR_COLS_SECOND = 256
+PASS_MAJOR = 3
+HALF = SPAN // 2
+TAIL_VECTOR_COLS = 160
+
+
+def tile_patch_embed_token_planes_g2_kernel(tc, patches, w_embed, bias, row_pos, col_pos, out_0, out_1, out_2):
+    nc = tc.nc
+    with ExitStack() as ctx:
+        keep = ctx.enter_context(tc.tile_pool(name="keep", bufs=1))
+        raw = ctx.enter_context(tc.tile_pool(name="raw", bufs=RAW_BUFS))
+        stage = ctx.enter_context(tc.tile_pool(name="stage", bufs=3))
+        psum_acc = ctx.enter_context(tc.psum_pool(name="psum", bufs=1))
+        ctx.enter_context(tc.manual_schedule())
+
+        ident = keep.tile([P, P], F32, name="ident")
+        make_identity(nc, ident[:])
+
+        x_raw, w_raw, x_grouped, w_grouped = {}, {}, {}, {}
+        x_codes, x_scales, w_codes, w_scales = {}, {}, {}, {}
+        row_in, col_in, row_sum, pos, acc, y = {}, {}, {}, {}, {}, {}
+        y_scales = keep.tile([P, D], U8, name="y_scales", align_bytes=64)
+
+        def load_x(n):
+            g, j = divmod(n, PASSES)
+            x_raw[n] = raw.tile([P, PACK, SPAN], BF16, name="x_raw", tag="x_raw")
+            src = patches[g * SPAN : (g + 1) * SPAN, j * SPAN : (j + 1) * SPAN]
+            nc.sync.dma_start(out=x_raw[n][:], in_=src.rearrange("(p t) k -> p t k", t=PACK))
+
+        def load_w(n):
+            h, j = divmod(n, PASSES)
+            w_raw[n] = raw.tile([P, PACK, SPAN], BF16, name="w_raw", tag="w_raw")
+            src = w_embed[j * SPAN : (j + 1) * SPAN, h * SPAN : (h + 1) * SPAN]
+            nc.sync.dma_start(out=w_raw[n][:], in_=src.rearrange("(p t) d -> p t d", t=PACK))
+
+        def load_row(h):
+            cols = slice(h * SPAN, (h + 1) * SPAN)
+            b = keep.tile([P, SPAN], BF16, name="bias%d" % h)
+            r = keep.tile([P, SPAN], BF16, name="row%d" % h)
+            nc.sync.dma_start(out=b[:], in_=bias[cols].partition_broadcast(P))
+            nc.sync.dma_start(out=r[:], in_=row_pos[:, cols].unsqueeze(1).broadcast_to([GH, P // GH, SPAN]))
+            row_in[h] = (b, r)
+
+        def load_col(h):
+            cols = slice(h * SPAN, (h + 1) * SPAN)
+            col_in[h] = keep.tile([P, PACK, SPAN], BF16, name="col%d" % h)
+            nc.sync.dma_start(out=col_in[h][:], in_=col_pos[:, cols].unsqueeze(0).broadcast_to([GH, GW, SPAN]))
+
+        def make_row(h):
+            b, r = row_in[h]
+            row_sum[h] = keep.tile([P, SPAN], F32, name="row_sum%d" % h)
+            nc.vector.tensor_tensor(out=row_sum[h][:], in0=r[:], in1=b[:], op=ADD)
+            pos[h] = keep.tile([P, PACK, SPAN], F32, name="pos%d" % h)
+
+        def make_pos(h, ts, cols):
+            count, width = ts.stop - ts.start, cols.stop - cols.start
+            spread = row_sum[h][:, cols].unsqueeze(1).broadcast_to([P, count, width])
+            nc.vector.tensor_tensor(out=pos[h][:, ts, cols], in0=col_in[h][:, ts, cols], in1=spread, op=ADD)
+
+        def bank(i, shape):
+            return psum_acc.tile(shape, F32, name="bank%d" % i, tag="bank%d" % i)
+
+        def turn_x(n):
+            words = x_raw[n][:].bitcast(F32)
+            x_grouped[n] = stage.tile([P, SPAN, PACK], BF16, name="x_grouped", tag="x_grouped", align_bytes=64)
+            dst = x_grouped[n][:].bitcast(F32).rearrange("p (t r) u -> p t r u", t=PACK)
+            for half in range(2):
+                xt = bank(4 + 2 * (n % 2) + half, [P, 2, 2, P])
+                for tt in range(2):
+                    for u in range(2):
+                        nc.tensor.transpose(xt[:, tt, u, :], words[:, 2 * half + tt, u :: 2], ident[:])
+                nc.scalar.copy(out=dst[:, 2 * half : 2 * half + 2], in_=xt[:].rearrange("p t u r -> p t r u"))
+
+        def interleave(copy, dst, src):
+            copy(out=dst.rearrange("p (c i) t -> p c t i", i=4), in_=src.rearrange("p t (c i) -> p c t i", i=4))
+
+        def group_w(n):
+            split = W_VECTOR_COLS_FIRST if n < PASSES else W_VECTOR_COLS_SECOND
+            w_grouped[n] = stage.tile([P, SPAN, PACK], BF16, name="w_grouped", tag="w_grouped", align_bytes=64)
+            interleave(nc.vector.tensor_copy, w_grouped[n][:, :split, :], w_raw[n][:, :, :split])
+            interleave(nc.scalar.copy, w_grouped[n][:, split:, :], w_raw[n][:, :, split:])
+
+        def quantize(name, grouped):
+            codes = keep.tile([P, SPAN], U32, name=name + "_codes", align_bytes=64)
+            scales = keep.tile([P, SPAN], U8, name=name + "_scales", align_bytes=64)
+            nc.vector.quantize_mx(
+                out=codes[:].bitcast(FP8X4), scales=scales[:], in_=grouped[:].rearrange("p c t -> p (c t)")
+            )
+            return codes, scales
+
+        def quantize_x(n):
+            x_codes[n], x_scales[n] = quantize("x%d" % n, x_grouped[n])
+
+        def quantize_w(n):
+            w_codes[n], w_scales[n] = quantize("w%d" % n, w_grouped[n])
+
+        def multiply(dst, g, h, j, t, cols):
+            tok = slice(t * P, (t + 1) * P)
+            nc.tensor.matmul_mx(
+                out=dst,
+                lhsT=x_codes[g * PASSES + j][:, tok].bitcast(FP8X4),
+                lhsT_scale=x_scales[g * PASSES + j][:, tok],
+                rhs=w_codes[h * PASSES + j][:, cols].bitcast(FP8X4),
+                rhs_scale=w_scales[h * PASSES + j][:, cols],
+                start=(j == 0),
+                stop=(j == PASSES - 1),
+            )
+
+        def multiply_pass(g, h, j, first_bank):
+            for t in range(PACK):
+                if j == 0:
+                    acc[g, h, t] = bank(first_bank + t, [P, SPAN])
+                multiply(acc[g, h, t][:], g, h, j, t, whole)
+
+        def add_pos(g, h, t):
+            nc.vector.tensor_tensor(out=y[g, h][:, t, :], in0=acc[g, h, t][:], in1=pos[h][:, t, :], op=ADD)
+
+        def store_y(g, h, cols, ts=slice(0, PACK)):
+            dst = out_0[g * SPAN : (g + 1) * SPAN, h * SPAN : (h + 1) * SPAN].rearrange("(p t) d -> p t d", t=PACK)
+            nc.sync.dma_start(out=dst[:, ts, cols], in_=y[g, h][:, ts, cols])
+
+        def group_y(g, h, cols, copy):
+            interleave(copy, y_grouped[g, h][:, cols, :], y[g, h][:, :, cols])
+
+        def quantize_y(g, h, cols):
+            wide = slice(h * SPAN + cols.start, h * SPAN + cols.stop)
+            nc.vector.quantize_mx(
+                out=y_codes[g][:, wide].bitcast(FP8X4),
+                scales=y_scales[4 * g :, wide],
+                in_=y_grouped[g, h][:, cols, :].rearrange("p c t -> p (c t)"),
+            )
+            dst = out_1[g].rearrange("p d t -> p (d t)").bitcast(I32)
+            nc.sync.dma_start(out=dst[:, wide], in_=y_codes[g][:, wide].bitcast(I32))
+
+        whole = slice(0, SPAN)
+        y_grouped, y_codes = {}, {}
+        for g in range(2):
+            y_codes[g] = keep.tile([P, D], U32, name="y_codes%d" % g, align_bytes=64)
+            for h in range(2):
+                y[g, h] = keep.tile([P, PACK, SPAN], F32, name="y%d%d" % (g, h))
+
+        def new_y_grouped(g, h):
+            y_grouped[g, h] = stage.tile([P, SPAN, PACK], BF16, name="y_grouped", tag="y_grouped", align_bytes=64, bufs=2)
+
+        def piece(g, c, ts, bank_index):
+            cols = slice(c * HALF, (c + 1) * HALF)
+            part = bank(bank_index, [P, ts.stop - ts.start, HALF])
+            for t in range(ts.start, ts.stop):
+                for j in range(PASSES):
+                    multiply(part[:, t - ts.start, :], g, 1, j, t, cols)
+            return part
+
+        def add_piece(g, c, ts, part):
+            cols = slice(c * HALF, (c + 1) * HALF)
+            nc.vector.tensor_tensor(out=y[g, 1][:, ts, cols], in0=part[:], in1=pos[1][:, ts, cols], op=ADD)
+
+        load_x(0)
+        load_x(1)
+        for j in range(PASSES):
+            load_w(j)
+            if j == PASSES - 1:
+                load_row(0)
+                load_col(0)
+            load_x(j + 2)
+
+        turn_x(0)
+        turn_x(1)
+        group_w(0)
+        quantize_x(0)
+        quantize_w(0)
+        for j in range(PASSES - 1):
+            group_w(j + 1)
+            turn_x(j + 2)
+            quantize_x(j + 1)
+            quantize_w(j + 1)
+            multiply_pass(0, 0, j, 0)
+        multiply_pass(0, 0, PASSES - 1, 0)
+        load_x(8)
+        load_x(9)
+        load_w(6)
+        load_x(10)
+        load_x(11)
+        load_w(7)
+        for m in range(8, CHUNKS):
+            load_w(m)
+        load_row(1)
+        load_col(1)
+
+        make_row(0)
+        quantize_x(6)
+        turn_x(7)
+        for t in range(PACK):
+            make_pos(0, slice(t, t + 1), whole)
+            if t > 0:
+                add_pos(0, 0, t - 1)
+        turn_x(8)
+        add_pos(0, 0, PACK - 1)
+        quantize_x(7)
+        store_y(0, 0, whole)
+        turn_x(9)
+        quantize_x(8)
+        group_w(6)
+        quantize_x(9)
+        multiply_pass(1, 0, 0, 0)
+        multiply_pass(1, 0, 1, 0)
+        turn_x(10)
+        quantize_w(6)
+        group_w(7)
+        quantize_x(10)
+        turn_x(11)
+        quantize_w(7)
+        group_w(8)
+        quantize_x(11)
+        for j in range(2, PASSES):
+            multiply_pass(1, 0, j, 0)
+        group_w(9)
+        quantize_w(8)
+        group_w(10)
+        quantize_w(9)
+        add_pos(1, 0, 0)
+        group_w(11)
+        quantize_w(10)
+        add_pos(1, 0, 1)
+        make_row(1)
+        quantize_w(11)
+        add_pos(1, 0, 2)
+        add_pos(1, 0, 3)
+        store_y(1, 0, whole)
+
+        low, high = slice(0, 2), slice(2, 4)
+        halves = [slice(0, HALF), slice(HALF, SPAN)]
+        new_y_grouped(0, 0)
+        group_y(0, 0, whole, nc.scalar.copy)
+        new_y_grouped(1, 0)
+        group_y(1, 0, whole, nc.scalar.copy)
+        for j in range(PASS_MAJOR):
+            multiply_pass(0, 1, j, 4)
+        make_pos(1, slice(0, 1), whole)
+        for t in range(PACK):
+            for j in range(PASS_MAJOR, PASSES):
+                multiply(acc[0, 1, t][:], 0, 1, j, t, whole)
+            if t + 1 < PACK:
+                make_pos(1, slice(t + 1, t + 2), whole)
+            add_pos(0, 1, t)
+            store_y(0, 1, whole, slice(t, t + 1))
+            if t == 1:
+                quantize_y(0, 0, whole)
+        quantize_y(1, 0, whole)
+        new_y_grouped(0, 1)
+        group_y(0, 1, whole, nc.scalar.copy)
+
+        parts = [piece(1, 0, low, 0), piece(1, 0, high, 1)]
+        add_piece(1, 0, low, parts[0])
+        add_piece(1, 0, high, parts[1])
+        store_y(1, 1, halves[0])
+        new_y_grouped(1, 1)
+        group_y(1, 1, halves[0], nc.scalar.copy)
+        quantize_y(0, 1, whole)
+
+        for t in range(PACK):
+            one = slice(t, t + 1)
+            add_piece(1, 1, one, piece(1, 1, one, 2 + t))
+            if t == 2:
+                quantize_y(1, 1, halves[0])
+            if t % 2 == 1:
+                store_y(1, 1, halves[1], slice(t - 1, t + 1))
+        cut = HALF + TAIL_VECTOR_COLS
+        group_y(1, 1, slice(HALF, cut), nc.vector.tensor_copy)
+        group_y(1, 1, slice(cut, SPAN), nc.scalar.copy)
+        quantize_y(1, 1, halves[1])
+        scale_rows = out_2.bitcast(I32)
+        for q in range(4):
+            queue = nc.sync if q % 2 == 0 else nc.scalar
+            queue.dma_start(
+                out=scale_rows[:, 4 * q : 4 * q + 4, :], in_=y_scales[32 * q : 32 * q + 8, :].bitcast(I32)
+            )

@@ -23,6 +23,10 @@ RAW_BUFS = 8
 W_VECTOR_COLS_FIRST = 320
 W_VECTOR_COLS_SECOND = 256
 PASS_MAJOR = 3
+WORD_BLOCKS = D // (2 * P)
+TABLE_ROWS = 64
+W_VECTOR_COLS_HEAD = 384
+COLS_AT = 3
 HALF = SPAN // 2
 TAIL_VECTOR_COLS = 160
 
@@ -41,7 +45,16 @@ def tile_patch_embed_token_planes_g2_kernel(tc, patches, w_embed, bias, row_pos,
 
         x_raw, w_raw, x_grouped, w_grouped = {}, {}, {}, {}
         x_codes, x_scales, w_codes, w_scales = {}, {}, {}, {}
-        row_in, col_in, row_sum, pos, acc, y = {}, {}, {}, {}, {}, {}
+        pos, acc, y = {}, {}, {}
+        tables = keep.tile([P, D], BF16, name="tables")
+        tables_t = keep.tile([P, WORD_BLOCKS, TABLE_ROWS], F32, name="tables_t")
+        row_t = keep.tile([P, WORD_BLOCKS, P], F32, name="row_t")
+        col_t = keep.tile([P, PACK, WORD_BLOCKS, P], F32, name="col_t")
+        bias_all = keep.tile([P, D], BF16, name="bias_all")
+        row_sum = keep.tile([P, D], F32, name="row_sum")
+        col_late = keep.tile([P, PACK, SPAN], BF16, name="col_late")
+        for h in range(2):
+            pos[h] = keep.tile([P, PACK, SPAN], F32, name="pos%d" % h)
         y_scales = keep.tile([P, D], U8, name="y_scales", align_bytes=64)
 
         def load_x(n):
@@ -56,29 +69,59 @@ def tile_patch_embed_token_planes_g2_kernel(tc, patches, w_embed, bias, row_pos,
             src = w_embed[j * SPAN : (j + 1) * SPAN, h * SPAN : (h + 1) * SPAN]
             nc.sync.dma_start(out=w_raw[n][:], in_=src.rearrange("(p t) d -> p t d", t=PACK))
 
-        def load_row(h):
-            cols = slice(h * SPAN, (h + 1) * SPAN)
-            b = keep.tile([P, SPAN], BF16, name="bias%d" % h)
-            r = keep.tile([P, SPAN], BF16, name="row%d" % h)
-            nc.sync.dma_start(out=b[:], in_=bias[cols].partition_broadcast(P))
-            nc.sync.dma_start(out=r[:], in_=row_pos[:, cols].unsqueeze(1).broadcast_to([GH, P // GH, SPAN]))
-            row_in[h] = (b, r)
+        def load_tables():
+            nc.vector.memset(tables[:].bitcast(I32), 0)
+            nc.scalar.dma_start(out=tables[0:GW, :], in_=col_pos.rearrange("(c t) d -> t c d", t=PACK))
+            nc.scalar.dma_start(out=tables[GW : GW + GH, :], in_=row_pos)
+            nc.scalar.dma_start(out=tables[GW + GH : GW + GH + 1, :], in_=bias.unsqueeze(0))
 
-        def load_col(h):
-            cols = slice(h * SPAN, (h + 1) * SPAN)
-            col_in[h] = keep.tile([P, PACK, SPAN], BF16, name="col%d" % h)
-            nc.sync.dma_start(out=col_in[h][:], in_=col_pos[:, cols].unsqueeze(0).broadcast_to([GH, GW, SPAN]))
+        def turn_tables():
+            words = tables[:].bitcast(F32)
+            turned = bank(0, [P, WORD_BLOCKS, P])
+            for b in range(WORD_BLOCKS):
+                nc.tensor.transpose(turned[:, b, :], words[:, b * P : (b + 1) * P], ident[:])
+            nc.scalar.copy(out=tables_t[:], in_=turned[:, :, :TABLE_ROWS])
 
-        def make_row(h):
-            b, r = row_in[h]
-            row_sum[h] = keep.tile([P, SPAN], F32, name="row_sum%d" % h)
-            nc.vector.tensor_tensor(out=row_sum[h][:], in0=r[:], in1=b[:], op=ADD)
-            pos[h] = keep.tile([P, PACK, SPAN], F32, name="pos%d" % h)
+        def spread_tables():
+            rows = tables_t[:, :, GW : GW + GH].unsqueeze(3).broadcast_to([P, WORD_BLOCKS, GH, P // GH])
+            nc.vector.tensor_copy(out=row_t[:].rearrange("n b (r c) -> n b r c", r=GH), in_=rows)
+            for t in range(PACK):
+                cols = tables_t[:, :, t * 8 : (t + 1) * 8].unsqueeze(2).broadcast_to([P, WORD_BLOCKS, GH, P // GH])
+                nc.vector.tensor_copy(out=col_t[:, t].rearrange("n b (r c) -> n b r c", r=GH), in_=cols)
 
-        def make_pos(h, ts, cols):
-            count, width = ts.stop - ts.start, cols.stop - cols.start
-            spread = row_sum[h][:, cols].unsqueeze(1).broadcast_to([P, count, width])
-            nc.vector.tensor_tensor(out=pos[h][:, ts, cols], in0=col_in[h][:, ts, cols], in1=spread, op=ADD)
+        def turn_bias():
+            turned = bank(1, [P, WORD_BLOCKS, P])
+            for b in range(WORD_BLOCKS):
+                column = tables_t[:, b, GW + GH : GW + GH + 1].to_broadcast([P, P])
+                nc.tensor.transpose(turned[:, b, :], column, ident[:])
+            nc.scalar.copy(out=bias_all[:].bitcast(F32), in_=turned[:].rearrange("p b n -> p (b n)"))
+
+        def turn_rows():
+            turned = bank(3, [P, WORD_BLOCKS, P])
+            for b in range(WORD_BLOCKS):
+                nc.tensor.transpose(turned[:, b, :], row_t[:, b, :], ident[:])
+            return turned[:].rearrange("p b n -> p (b n)").bitcast(BF16)
+
+        def turn_cols(h):
+            pair = next_pair()
+            turned = []
+            for half in range(2):
+                ct = bank(pair + half, [P, 2, 2, P])
+                for tt in range(2):
+                    for b in range(2):
+                        nc.tensor.transpose(ct[:, tt, b, :], col_t[:, 2 * half + tt, 2 * h + b, :], ident[:])
+                turned.append(ct[:].rearrange("p t b n -> p t (b n)"))
+            return turned
+
+        def make_pos(h, ts, col):
+            spread = row_sum[:, h * SPAN : (h + 1) * SPAN].unsqueeze(1).broadcast_to([P, ts.stop - ts.start, SPAN])
+            nc.vector.tensor_tensor(out=pos[h][:, ts, :], in0=col, in1=spread, op=ADD)
+
+        pairs_used = []
+
+        def next_pair():
+            pairs_used.append(0)
+            return 4 + 2 * (len(pairs_used) % 2)
 
         def bank(i, shape):
             return psum_acc.tile(shape, F32, name="bank%d" % i, tag="bank%d" % i)
@@ -87,8 +130,9 @@ def tile_patch_embed_token_planes_g2_kernel(tc, patches, w_embed, bias, row_pos,
             words = x_raw[n][:].bitcast(F32)
             x_grouped[n] = stage.tile([P, SPAN, PACK], BF16, name="x_grouped", tag="x_grouped", align_bytes=64)
             dst = x_grouped[n][:].bitcast(F32).rearrange("p (t r) u -> p t r u", t=PACK)
+            pair = next_pair()
             for half in range(2):
-                xt = bank(4 + 2 * (n % 2) + half, [P, 2, 2, P])
+                xt = bank(pair + half, [P, 2, 2, P])
                 for tt in range(2):
                     for u in range(2):
                         nc.tensor.transpose(xt[:, tt, u, :], words[:, 2 * half + tt, u :: 2], ident[:])
@@ -98,7 +142,7 @@ def tile_patch_embed_token_planes_g2_kernel(tc, patches, w_embed, bias, row_pos,
             copy(out=dst.rearrange("p (c i) t -> p c t i", i=4), in_=src.rearrange("p t (c i) -> p c t i", i=4))
 
         def group_w(n):
-            split = W_VECTOR_COLS_FIRST if n < PASSES else W_VECTOR_COLS_SECOND
+            split = W_VECTOR_COLS_HEAD if n == 0 else W_VECTOR_COLS_FIRST if n < PASSES else W_VECTOR_COLS_SECOND
             w_grouped[n] = stage.tile([P, SPAN, PACK], BF16, name="w_grouped", tag="w_grouped", align_bytes=64)
             interleave(nc.vector.tensor_copy, w_grouped[n][:, :split, :], w_raw[n][:, :, :split])
             interleave(nc.scalar.copy, w_grouped[n][:, split:, :], w_raw[n][:, :, split:])
@@ -177,27 +221,35 @@ def tile_patch_embed_token_planes_g2_kernel(tc, patches, w_embed, bias, row_pos,
             cols = slice(c * HALF, (c + 1) * HALF)
             nc.vector.tensor_tensor(out=y[g, 1][:, ts, cols], in0=part[:], in1=pos[1][:, ts, cols], op=ADD)
 
+        low, high = slice(0, 2), slice(2, 4)
+        load_tables()
         load_x(0)
         load_x(1)
         for j in range(PASSES):
             load_w(j)
-            if j == PASSES - 1:
-                load_row(0)
-                load_col(0)
             load_x(j + 2)
 
+        turn_tables()
         turn_x(0)
-        turn_x(1)
+        spread_tables()
+        turn_bias()
         group_w(0)
+        turn_x(1)
+        rows = turn_rows()
         quantize_x(0)
         quantize_w(0)
+        nc.vector.tensor_tensor(out=row_sum[:], in0=rows, in1=bias_all[:], op=ADD)
         for j in range(PASSES - 1):
             group_w(j + 1)
             turn_x(j + 2)
+            if j == COLS_AT:
+                cols = turn_cols(0)
             quantize_x(j + 1)
             quantize_w(j + 1)
+            if j == COLS_AT:
+                make_pos(0, low, cols[0].bitcast(BF16))
+                make_pos(0, high, cols[1].bitcast(BF16))
             multiply_pass(0, 0, j, 0)
-        multiply_pass(0, 0, PASSES - 1, 0)
         load_x(8)
         load_x(9)
         load_w(6)
@@ -206,21 +258,21 @@ def tile_patch_embed_token_planes_g2_kernel(tc, patches, w_embed, bias, row_pos,
         load_w(7)
         for m in range(8, CHUNKS):
             load_w(m)
-        load_row(1)
-        load_col(1)
 
-        make_row(0)
-        quantize_x(6)
         turn_x(7)
-        for t in range(PACK):
-            make_pos(0, slice(t, t + 1), whole)
-            if t > 0:
-                add_pos(0, 0, t - 1)
-        turn_x(8)
-        add_pos(0, 0, PACK - 1)
+        multiply_pass(0, 0, PASSES - 1, 0)
+        quantize_x(6)
+        add_pos(0, 0, 0)
+        add_pos(0, 0, 1)
         quantize_x(7)
+        add_pos(0, 0, 2)
+        add_pos(0, 0, 3)
+        turn_x(8)
         store_y(0, 0, whole)
         turn_x(9)
+        cols = turn_cols(1)
+        nc.scalar.copy(out=col_late[:, low, :].bitcast(F32), in_=cols[0])
+        nc.scalar.copy(out=col_late[:, high, :].bitcast(F32), in_=cols[1])
         quantize_x(8)
         group_w(6)
         quantize_x(9)
@@ -244,13 +296,11 @@ def tile_patch_embed_token_planes_g2_kernel(tc, patches, w_embed, bias, row_pos,
         group_w(11)
         quantize_w(10)
         add_pos(1, 0, 1)
-        make_row(1)
         quantize_w(11)
         add_pos(1, 0, 2)
         add_pos(1, 0, 3)
         store_y(1, 0, whole)
 
-        low, high = slice(0, 2), slice(2, 4)
         halves = [slice(0, HALF), slice(HALF, SPAN)]
         new_y_grouped(0, 0)
         group_y(0, 0, whole, nc.scalar.copy)
@@ -258,12 +308,12 @@ def tile_patch_embed_token_planes_g2_kernel(tc, patches, w_embed, bias, row_pos,
         group_y(1, 0, whole, nc.scalar.copy)
         for j in range(PASS_MAJOR):
             multiply_pass(0, 1, j, 4)
-        make_pos(1, slice(0, 1), whole)
+        make_pos(1, slice(0, 1), col_late[:, 0:1, :])
         for t in range(PACK):
             for j in range(PASS_MAJOR, PASSES):
                 multiply(acc[0, 1, t][:], 0, 1, j, t, whole)
             if t + 1 < PACK:
-                make_pos(1, slice(t + 1, t + 2), whole)
+                make_pos(1, slice(t + 1, t + 2), col_late[:, t + 1 : t + 2, :])
             add_pos(0, 1, t)
             store_y(0, 1, whole, slice(t, t + 1))
             if t == 1:

@@ -19,14 +19,22 @@ PACK = 4
 SPAN = P * PACK
 PASSES = K // SPAN
 CHUNKS = 2 * PASSES
-RAW_BUFS = 8
-W_VECTOR_COLS_FIRST = 320
-W_VECTOR_COLS_SECOND = 256
+X_BUFS = 6
+STRIPS = 2 * PACK
+X_BANKS = STRIPS * PASSES // 2
+W_VECTOR_COLS_FIRST = 256
+W_VECTOR_COLS_SECOND = 192
 PASS_MAJOR = 3
-WORD_BLOCKS = D // (2 * P)
-TABLE_ROWS = 64
+PASS_MAJOR_FIRST = 4
+VECTOR_EVERY = 100
+W0_AT = 16
+W1_AT = 21
 W_VECTOR_COLS_HEAD = 384
-COLS_AT = 3
+COL_AT = [3, 6, 9, 12]
+W_BEFORE_ADDS = 8
+WORD_BLOCKS = D // (2 * P)
+COL_END = 2 * GW
+ROW_END = COL_END + 2 * GH
 HALF = SPAN // 2
 TAIL_VECTOR_COLS = 160
 
@@ -35,117 +43,120 @@ def tile_patch_embed_token_planes_g2_kernel(tc, patches, w_embed, bias, row_pos,
     nc = tc.nc
     with ExitStack() as ctx:
         keep = ctx.enter_context(tc.tile_pool(name="keep", bufs=1))
-        raw = ctx.enter_context(tc.tile_pool(name="raw", bufs=RAW_BUFS))
+        raw = ctx.enter_context(tc.tile_pool(name="raw", bufs=PASSES))
         stage = ctx.enter_context(tc.tile_pool(name="stage", bufs=3))
         psum_acc = ctx.enter_context(tc.psum_pool(name="psum", bufs=1))
         ctx.enter_context(tc.manual_schedule())
 
         ident = keep.tile([P, P], F32, name="ident")
-        make_identity(nc, ident[:])
 
         x_raw, w_raw, x_grouped, w_grouped = {}, {}, {}, {}
-        x_codes, x_scales, w_codes, w_scales = {}, {}, {}, {}
-        pos, acc, y = {}, {}, {}
-        tables = keep.tile([P, D], BF16, name="tables")
-        tables_t = keep.tile([P, WORD_BLOCKS, TABLE_ROWS], F32, name="tables_t")
+        w_codes, w_scales = {}, {}
+        acc, y = {}, {}
+        tables = keep.tile([P, SPAN], BF16, name="tables")
+        rest_t = keep.tile([P, 2, 2 * GH + 2], F32, name="rest_t")
+        cols_t = keep.tile([P, 2, 8, 8], F32, name="cols_t")
         row_t = keep.tile([P, WORD_BLOCKS, P], F32, name="row_t")
         col_t = keep.tile([P, PACK, WORD_BLOCKS, P], F32, name="col_t")
         bias_all = keep.tile([P, D], BF16, name="bias_all")
         row_sum = keep.tile([P, D], F32, name="row_sum")
-        col_late = keep.tile([P, PACK, SPAN], BF16, name="col_late")
-        for h in range(2):
-            pos[h] = keep.tile([P, PACK, SPAN], F32, name="pos%d" % h)
+        pos = keep.tile([P, PACK, D], F32, name="pos")
+        x_codes = keep.tile([P, STRIPS * PASSES * P], U32, name="x_codes", align_bytes=64)
+        x_scales = keep.tile([P, STRIPS * PASSES * P], U8, name="x_scales", align_bytes=64)
         y_scales = keep.tile([P, D], U8, name="y_scales", align_bytes=64)
 
-        def load_x(n):
-            g, j = divmod(n, PASSES)
-            x_raw[n] = raw.tile([P, PACK, SPAN], BF16, name="x_raw", tag="x_raw")
-            src = patches[g * SPAN : (g + 1) * SPAN, j * SPAN : (j + 1) * SPAN]
-            nc.sync.dma_start(out=x_raw[n][:], in_=src.rearrange("(p t) k -> p t k", t=PACK))
+        def load_x(s, ks=slice(0, K)):
+            g, t = divmod(s, PACK)
+            width = ks.stop - ks.start
+            tile = raw.tile([P, width], BF16, name="x_raw", tag="x_raw", bufs=X_BUFS)
+            src = patches[g * SPAN : (g + 1) * SPAN, ks].rearrange("(p t) k -> p t k", t=PACK)
+            nc.sync.dma_start(out=tile[:], in_=src[:, t, :])
+            for j in range(ks.start // SPAN, ks.stop // SPAN):
+                x_raw[s, j] = tile[:].bitcast(F32)[:, (j * SPAN - ks.start) // 2 : ((j + 1) * SPAN - ks.start) // 2]
 
         def load_w(n):
             h, j = divmod(n, PASSES)
-            w_raw[n] = raw.tile([P, PACK, SPAN], BF16, name="w_raw", tag="w_raw")
+            w_raw[n] = raw.tile([P, PACK, SPAN], BF16, name="w_raw", tag="w_raw", bufs=PASSES)
             src = w_embed[j * SPAN : (j + 1) * SPAN, h * SPAN : (h + 1) * SPAN]
             nc.sync.dma_start(out=w_raw[n][:], in_=src.rearrange("(p t) d -> p t d", t=PACK))
 
         def load_tables():
-            nc.vector.memset(tables[:].bitcast(I32), 0)
-            nc.scalar.dma_start(out=tables[0:GW, :], in_=col_pos.rearrange("(c t) d -> t c d", t=PACK))
-            nc.scalar.dma_start(out=tables[GW : GW + GH, :], in_=row_pos)
-            nc.scalar.dma_start(out=tables[GW + GH : GW + GH + 1, :], in_=bias.unsqueeze(0))
+            nc.gpsimd.memset(tables[ROW_END:P, :].bitcast(I32), 0)
+            nc.sync.dma_start(out=tables[0:COL_END, :], in_=col_pos.rearrange("c (h d) -> (c h) d", h=2))
+            nc.sync.dma_start(out=tables[COL_END:ROW_END, :], in_=row_pos.rearrange("r (h d) -> (r h) d", h=2))
+            nc.sync.dma_start(out=tables[ROW_END : ROW_END + 2, :], in_=bias.rearrange("(h d) -> h d", h=2))
 
         def turn_tables():
             words = tables[:].bitcast(F32)
-            turned = bank(0, [P, WORD_BLOCKS, P])
-            for b in range(WORD_BLOCKS):
+            turned = bank(next_bank(), [P, 2, P])
+            for b in range(2):
                 nc.tensor.transpose(turned[:, b, :], words[:, b * P : (b + 1) * P], ident[:])
-            nc.scalar.copy(out=tables_t[:], in_=turned[:, :, :TABLE_ROWS])
+            nc.scalar.copy(out=rest_t[:], in_=turned[:, :, COL_END : ROW_END + 2])
+            nc.scalar.copy(out=cols_t[:], in_=turned[:, :, 0:COL_END].rearrange("n b (c u) -> n b u c", c=8))
 
         def spread_tables():
-            rows = tables_t[:, :, GW : GW + GH].unsqueeze(3).broadcast_to([P, WORD_BLOCKS, GH, P // GH])
-            nc.vector.tensor_copy(out=row_t[:].rearrange("n b (r c) -> n b r c", r=GH), in_=rows)
-            for t in range(PACK):
-                cols = tables_t[:, :, t * 8 : (t + 1) * 8].unsqueeze(2).broadcast_to([P, WORD_BLOCKS, GH, P // GH])
-                nc.vector.tensor_copy(out=col_t[:, t].rearrange("n b (r c) -> n b r c", r=GH), in_=cols)
+            for h in range(2):
+                rows = rest_t[:, :, h : 2 * GH : 2].unsqueeze(3).broadcast_to([P, 2, GH, P // GH])
+                nc.vector.tensor_copy(out=row_t[:, 2 * h : 2 * h + 2].rearrange("n b (r c) -> n b r c", r=GH), in_=rows)
+            for b in range(2):
+                cols = cols_t[:, b].unsqueeze(2).broadcast_to([P, 8, GH, P // GH])
+                dst = col_t[:].rearrange("n t (h b) (r c) -> n b (t h) r c", b=2, r=GH)
+                nc.vector.tensor_copy(out=dst[:, b], in_=cols)
 
         def turn_bias():
-            turned = bank(1, [P, WORD_BLOCKS, P])
-            for b in range(WORD_BLOCKS):
-                column = tables_t[:, b, GW + GH : GW + GH + 1].to_broadcast([P, P])
-                nc.tensor.transpose(turned[:, b, :], column, ident[:])
+            turned = bank(next_bank(), [P, WORD_BLOCKS, P])
+            for h in range(2):
+                for b in range(2):
+                    column = rest_t[:, b, 2 * GH + h : 2 * GH + h + 1].to_broadcast([P, P])
+                    nc.tensor.transpose(turned[:, 2 * h + b, :], column, ident[:])
             nc.scalar.copy(out=bias_all[:].bitcast(F32), in_=turned[:].rearrange("p b n -> p (b n)"))
 
         def turn_rows():
-            turned = bank(3, [P, WORD_BLOCKS, P])
+            turned = bank(next_bank(), [P, WORD_BLOCKS, P])
             for b in range(WORD_BLOCKS):
                 nc.tensor.transpose(turned[:, b, :], row_t[:, b, :], ident[:])
             return turned[:].rearrange("p b n -> p (b n)").bitcast(BF16)
 
-        def turn_cols(h):
-            pair = next_pair()
-            turned = []
-            for half in range(2):
-                ct = bank(pair + half, [P, 2, 2, P])
-                for tt in range(2):
-                    for b in range(2):
-                        nc.tensor.transpose(ct[:, tt, b, :], col_t[:, 2 * half + tt, 2 * h + b, :], ident[:])
-                turned.append(ct[:].rearrange("p t b n -> p t (b n)"))
-            return turned
+        def turn_cols(t):
+            turned = bank(next_bank(), [P, WORD_BLOCKS, P])
+            for b in range(WORD_BLOCKS):
+                nc.tensor.transpose(turned[:, b, :], col_t[:, t, b, :], ident[:])
+            return turned[:].rearrange("p b n -> p (b n)").bitcast(BF16)
 
-        def make_pos(h, ts, col):
-            spread = row_sum[:, h * SPAN : (h + 1) * SPAN].unsqueeze(1).broadcast_to([P, ts.stop - ts.start, SPAN])
-            nc.vector.tensor_tensor(out=pos[h][:, ts, :], in0=col, in1=spread, op=ADD)
+        def make_pos(t, col):
+            nc.vector.tensor_tensor(out=pos[:, t, :], in0=col, in1=row_sum[:], op=ADD)
 
-        pairs_used = []
+        banks_used = []
+        wide_rotation = [True]
 
-        def next_pair():
-            pairs_used.append(0)
-            return 4 + 2 * (len(pairs_used) % 2)
+        def next_bank():
+            banks_used.append(0)
+            return len(banks_used) % 8 if wide_rotation else 4 + len(banks_used) % 4
 
         def bank(i, shape):
             return psum_acc.tile(shape, F32, name="bank%d" % i, tag="bank%d" % i)
 
-        def turn_x(n):
-            words = x_raw[n][:].bitcast(F32)
-            x_grouped[n] = stage.tile([P, SPAN, PACK], BF16, name="x_grouped", tag="x_grouped", align_bytes=64)
-            dst = x_grouped[n][:].bitcast(F32).rearrange("p (t r) u -> p t r u", t=PACK)
-            pair = next_pair()
-            for half in range(2):
-                xt = bank(pair + half, [P, 2, 2, P])
-                for tt in range(2):
-                    for u in range(2):
-                        nc.tensor.transpose(xt[:, tt, u, :], words[:, 2 * half + tt, u :: 2], ident[:])
-                nc.scalar.copy(out=dst[:, 2 * half : 2 * half + 2], in_=xt[:].rearrange("p t u r -> p t r u"))
+        def turn_x(b):
+            s, jj = divmod(b, PASSES // 2)
+            if b % 2 == 0:
+                x_grouped[b // 2] = stage.tile([P, SPAN, PACK], BF16, name="x_grouped", tag="x_grouped", align_bytes=64)
+            dst = x_grouped[b // 2][:].bitcast(F32).rearrange("p (b j r) u -> p b j r u", b=2, j=2)
+            xt = bank(next_bank(), [P, 2, 2, P])
+            for j in range(2):
+                for u in range(2):
+                    nc.tensor.transpose(xt[:, j, u, :], x_raw[s, 2 * jj + j][:, u :: 2], ident[:])
+            copy = nc.vector.tensor_copy if b % VECTOR_EVERY == VECTOR_EVERY - 1 else nc.scalar.copy
+            copy(out=dst[:, b % 2], in_=xt[:].rearrange("p j u r -> p j r u"))
 
         def interleave(copy, dst, src):
             copy(out=dst.rearrange("p (c i) t -> p c t i", i=4), in_=src.rearrange("p t (c i) -> p c t i", i=4))
 
         def group_w(n):
-            split = W_VECTOR_COLS_HEAD if n == 0 else W_VECTOR_COLS_FIRST if n < PASSES else W_VECTOR_COLS_SECOND
+            split = W_VECTOR_COLS_HEAD if n < 2 else W_VECTOR_COLS_FIRST if n <= W_BEFORE_ADDS else W_VECTOR_COLS_SECOND
             w_grouped[n] = stage.tile([P, SPAN, PACK], BF16, name="w_grouped", tag="w_grouped", align_bytes=64)
             interleave(nc.vector.tensor_copy, w_grouped[n][:, :split, :], w_raw[n][:, :, :split])
-            interleave(nc.scalar.copy, w_grouped[n][:, split:, :], w_raw[n][:, :, split:])
+            if split < SPAN:
+                interleave(nc.scalar.copy, w_grouped[n][:, split:, :], w_raw[n][:, :, split:])
 
         def quantize(name, grouped):
             codes = keep.tile([P, SPAN], U32, name=name + "_codes", align_bytes=64)
@@ -156,17 +167,23 @@ def tile_patch_embed_token_planes_g2_kernel(tc, patches, w_embed, bias, row_pos,
             return codes, scales
 
         def quantize_x(n):
-            x_codes[n], x_scales[n] = quantize("x%d" % n, x_grouped[n])
+            cols = slice(n * SPAN, (n + 1) * SPAN)
+            nc.vector.quantize_mx(
+                out=x_codes[:, cols].bitcast(FP8X4),
+                scales=x_scales[:, cols],
+                in_=x_grouped[n][:].rearrange("p c t -> p (c t)"),
+            )
 
         def quantize_w(n):
             w_codes[n], w_scales[n] = quantize("w%d" % n, w_grouped[n])
 
         def multiply(dst, g, h, j, t, cols):
-            tok = slice(t * P, (t + 1) * P)
+            first = ((g * PACK + t) * PASSES + j) * P
+            tok = slice(first, first + P)
             nc.tensor.matmul_mx(
                 out=dst,
-                lhsT=x_codes[g * PASSES + j][:, tok].bitcast(FP8X4),
-                lhsT_scale=x_scales[g * PASSES + j][:, tok],
+                lhsT=x_codes[:, tok].bitcast(FP8X4),
+                lhsT_scale=x_scales[:, tok],
                 rhs=w_codes[h * PASSES + j][:, cols].bitcast(FP8X4),
                 rhs_scale=w_scales[h * PASSES + j][:, cols],
                 start=(j == 0),
@@ -180,7 +197,7 @@ def tile_patch_embed_token_planes_g2_kernel(tc, patches, w_embed, bias, row_pos,
                 multiply(acc[g, h, t][:], g, h, j, t, whole)
 
         def add_pos(g, h, t):
-            nc.vector.tensor_tensor(out=y[g, h][:, t, :], in0=acc[g, h, t][:], in1=pos[h][:, t, :], op=ADD)
+            nc.vector.tensor_tensor(out=y[g, h][:, t, :], in0=acc[g, h, t][:], in1=pos[:, t, h * SPAN : (h + 1) * SPAN], op=ADD)
 
         def store_y(g, h, cols, ts=slice(0, PACK)):
             dst = out_0[g * SPAN : (g + 1) * SPAN, h * SPAN : (h + 1) * SPAN].rearrange("(p t) d -> p t d", t=PACK)
@@ -219,86 +236,84 @@ def tile_patch_embed_token_planes_g2_kernel(tc, patches, w_embed, bias, row_pos,
 
         def add_piece(g, c, ts, part):
             cols = slice(c * HALF, (c + 1) * HALF)
-            nc.vector.tensor_tensor(out=y[g, 1][:, ts, cols], in0=part[:], in1=pos[1][:, ts, cols], op=ADD)
+            nc.vector.tensor_tensor(out=y[g, 1][:, ts, cols], in0=part[:], in1=pos[:, ts, SPAN + c * HALF : SPAN + (c + 1) * HALF], op=ADD)
 
         low, high = slice(0, 2), slice(2, 4)
         load_tables()
-        load_x(0)
-        load_x(1)
-        for j in range(PASSES):
-            load_w(j)
-            load_x(j + 2)
+        make_identity(nc, ident[:])
+        load_x(0, slice(0, K // 3))
+        load_x(0, slice(K // 3, K))
+        for s in range(1, X_BUFS - 1):
+            load_x(s)
 
         turn_tables()
-        turn_x(0)
         spread_tables()
         turn_bias()
-        group_w(0)
-        turn_x(1)
-        rows = turn_rows()
-        quantize_x(0)
-        quantize_w(0)
-        nc.vector.tensor_tensor(out=row_sum[:], in0=rows, in1=bias_all[:], op=ADD)
-        for j in range(PASSES - 1):
-            group_w(j + 1)
-            turn_x(j + 2)
-            if j == COLS_AT:
-                cols = turn_cols(0)
-            quantize_x(j + 1)
-            quantize_w(j + 1)
-            if j == COLS_AT:
-                make_pos(0, low, cols[0].bitcast(BF16))
-                make_pos(0, high, cols[1].bitcast(BF16))
-            multiply_pass(0, 0, j, 0)
-        load_x(8)
-        load_x(9)
-        load_w(6)
-        load_x(10)
-        load_x(11)
-        load_w(7)
-        for m in range(8, CHUNKS):
-            load_w(m)
-
-        turn_x(7)
-        multiply_pass(0, 0, PASSES - 1, 0)
-        quantize_x(6)
-        add_pos(0, 0, 0)
-        add_pos(0, 0, 1)
-        quantize_x(7)
-        add_pos(0, 0, 2)
-        add_pos(0, 0, 3)
-        turn_x(8)
+        for b in range(X_BANKS):
+            if b == 3:
+                load_x(5)
+                load_w(0)
+                load_x(6)
+                load_w(1)
+            if b == 6:
+                load_x(7)
+                for m in range(2, PASSES):
+                    load_w(m)
+            if b == 1:
+                rows = turn_rows()
+                nc.vector.tensor_tensor(out=row_sum[:], in0=rows, in1=bias_all[:], op=ADD)
+            if b == 17:
+                wide_rotation.clear()
+            for t in range(PACK):
+                if COL_AT[t] == b:
+                    make_pos(t, turn_cols(t))
+            if b == W0_AT:
+                group_w(0)
+            if b == W1_AT:
+                group_w(1)
+            if b == 21:
+                multiply_pass(0, 0, 0, 0)
+            turn_x(b)
+            if b == W0_AT + 1:
+                quantize_w(0)
+            if b == W1_AT + 1:
+                quantize_w(1)
+            if b % 2 == 0 and b > 0:
+                quantize_x(b // 2 - 1)
+        group_w(2)
+        quantize_x(X_BANKS // 2 - 1)
+        for m in range(2, W_BEFORE_ADDS):
+            if m == 2:
+                load_w(PASSES)
+            if m < PASSES:
+                load_w(PASSES + m - 1)
+            if m == PASSES - 1:
+                load_w(CHUNKS - 1)
+            group_w(m + 1)
+            quantize_w(m)
+        multiply_pass(0, 0, 1, 0)
+        multiply_pass(1, 0, 0, 4)
+        multiply_pass(1, 0, 1, 4)
+        for j in range(2, PASS_MAJOR_FIRST):
+            for g in range(2):
+                multiply_pass(g, 0, j, 4 * g)
+        for s in range(STRIPS):
+            g, t = divmod(s, PACK)
+            for j in range(PASS_MAJOR_FIRST, PASSES):
+                multiply(acc[g, 0, t][:], g, 0, j, t, whole)
+        for t in range(PACK):
+            add_pos(0, 0, t)
         store_y(0, 0, whole)
-        turn_x(9)
-        cols = turn_cols(1)
-        nc.scalar.copy(out=col_late[:, low, :].bitcast(F32), in_=cols[0])
-        nc.scalar.copy(out=col_late[:, high, :].bitcast(F32), in_=cols[1])
-        quantize_x(8)
-        group_w(6)
-        quantize_x(9)
-        multiply_pass(1, 0, 0, 0)
-        multiply_pass(1, 0, 1, 0)
-        turn_x(10)
-        quantize_w(6)
-        group_w(7)
-        quantize_x(10)
-        turn_x(11)
-        quantize_w(7)
-        group_w(8)
-        quantize_x(11)
-        for j in range(2, PASSES):
-            multiply_pass(1, 0, j, 0)
-        group_w(9)
-        quantize_w(8)
-        group_w(10)
-        quantize_w(9)
-        add_pos(1, 0, 0)
-        group_w(11)
-        quantize_w(10)
-        add_pos(1, 0, 1)
-        quantize_w(11)
-        add_pos(1, 0, 2)
-        add_pos(1, 0, 3)
+        done = 0
+        for m in range(W_BEFORE_ADDS, CHUNKS):
+            if m + 1 < CHUNKS:
+                group_w(m + 1)
+            else:
+                add_pos(1, 0, 0)
+                done = 1
+            quantize_w(m)
+        for t in range(done, PACK):
+            add_pos(1, 0, t)
         store_y(1, 0, whole)
 
         halves = [slice(0, HALF), slice(HALF, SPAN)]
@@ -307,13 +322,10 @@ def tile_patch_embed_token_planes_g2_kernel(tc, patches, w_embed, bias, row_pos,
         new_y_grouped(1, 0)
         group_y(1, 0, whole, nc.scalar.copy)
         for j in range(PASS_MAJOR):
-            multiply_pass(0, 1, j, 4)
-        make_pos(1, slice(0, 1), col_late[:, 0:1, :])
+            multiply_pass(0, 1, j, 0)
         for t in range(PACK):
             for j in range(PASS_MAJOR, PASSES):
                 multiply(acc[0, 1, t][:], 0, 1, j, t, whole)
-            if t + 1 < PACK:
-                make_pos(1, slice(t + 1, t + 2), col_late[:, t + 1 : t + 2, :])
             add_pos(0, 1, t)
             store_y(0, 1, whole, slice(t, t + 1))
             if t == 1:
@@ -322,7 +334,7 @@ def tile_patch_embed_token_planes_g2_kernel(tc, patches, w_embed, bias, row_pos,
         new_y_grouped(0, 1)
         group_y(0, 1, whole, nc.scalar.copy)
 
-        parts = [piece(1, 0, low, 0), piece(1, 0, high, 1)]
+        parts = [piece(1, 0, low, 4), piece(1, 0, high, 5)]
         add_piece(1, 0, low, parts[0])
         add_piece(1, 0, high, parts[1])
         store_y(1, 1, halves[0])
@@ -332,7 +344,7 @@ def tile_patch_embed_token_planes_g2_kernel(tc, patches, w_embed, bias, row_pos,
 
         for t in range(PACK):
             one = slice(t, t + 1)
-            add_piece(1, 1, one, piece(1, 1, one, 2 + t))
+            add_piece(1, 1, one, piece(1, 1, one, (6 + t) % 8))
             if t == 2:
                 quantize_y(1, 1, halves[0])
             if t % 2 == 1:

@@ -17,66 +17,95 @@ ADD = mybir.AluOpType.add
 P = 128
 PACK = 4
 SPAN = P * PACK
+HALF = SPAN // 2
 PASSES = K // SPAN
 CHUNKS = 2 * PASSES
-X_BUFS = 6
 STRIPS = 2 * PACK
-X_BANKS = STRIPS * PASSES // 2
-W_VECTOR_COLS_FIRST = 256
-W_VECTOR_COLS_SECOND = 192
-PASS_MAJOR = 3
-PASS_MAJOR_FIRST = 4
-VECTOR_EVERY = 100
-W0_AT = 16
-W1_AT = 21
-W_VECTOR_COLS_HEAD = 384
-COL_AT = [3, 6, 9, 12]
-W_BEFORE_ADDS = 8
-WORD_BLOCKS = D // (2 * P)
+BANKS = 8
+
+TURNS = PASSES // 2
+THIRD = K // TURNS
+WHOLE_STRIP_BUFS = 4
+CUT_STRIPS = (0, STRIPS - 2, STRIPS - 1)
+
 COL_END = 2 * GW
 ROW_END = COL_END + 2 * GH
-HALF = SPAN // 2
-TAIL_VECTOR_COLS = 160
+PER_ROW = P // GH
+
+VECTOR_COLS_EARLY = 384
+VECTOR_COLS_MIDDLE = 256
+VECTOR_COLS_LATE = 192
+VECTOR_COLS_LAST = 160
+CHUNKS_BEFORE_ADDS = 8
+PASS_MAJOR = 4
 
 
-def tile_patch_embed_token_planes_g2_kernel(tc, patches, w_embed, bias, row_pos, col_pos, out_0, out_1, out_2):
+def tile_patch_embed_token_planes_g2_kernel(
+    tc, patches, w_embed, bias, row_pos, col_pos, out_0, out_1, out_2
+):
     nc = tc.nc
     with ExitStack() as ctx:
         keep = ctx.enter_context(tc.tile_pool(name="keep", bufs=1))
         raw = ctx.enter_context(tc.tile_pool(name="raw", bufs=PASSES))
         stage = ctx.enter_context(tc.tile_pool(name="stage", bufs=3))
-        psum_acc = ctx.enter_context(tc.psum_pool(name="psum", bufs=1))
+        psum = ctx.enter_context(tc.psum_pool(name="psum", bufs=1))
         ctx.enter_context(tc.manual_schedule())
 
         ident = keep.tile([P, P], F32, name="ident")
-
-        x_raw, w_raw, x_grouped, w_grouped = {}, {}, {}, {}
-        w_codes, w_scales = {}, {}
-        acc, y = {}, {}
         tables = keep.tile([P, SPAN], BF16, name="tables")
-        rest_t = keep.tile([P, 2, 2 * GH + 2], F32, name="rest_t")
-        cols_t = keep.tile([P, 2, 8, 8], F32, name="cols_t")
-        row_t = keep.tile([P, WORD_BLOCKS, P], F32, name="row_t")
-        col_t = keep.tile([P, PACK, WORD_BLOCKS, P], F32, name="col_t")
-        bias_all = keep.tile([P, D], BF16, name="bias_all")
+        rows_turned = keep.tile([P, 2, 2 * GH + 2], F32, name="rows_turned")
+        cols_turned = keep.tile([P, 2, 2 * PACK, PER_ROW], F32, name="cols_turned")
+        row_bias = keep.tile([P, 2, GH, 4], F32, name="row_bias")
+        row_spread = keep.tile([P, 2, 4, P], F32, name="row_spread")
+        col_spread = keep.tile([P, PACK, 4, P], F32, name="col_spread")
         row_sum = keep.tile([P, D], F32, name="row_sum")
         pos = keep.tile([P, PACK, D], F32, name="pos")
         x_codes = keep.tile([P, STRIPS * PASSES * P], U32, name="x_codes", align_bytes=64)
         x_scales = keep.tile([P, STRIPS * PASSES * P], U8, name="x_scales", align_bytes=64)
         y_scales = keep.tile([P, D], U8, name="y_scales", align_bytes=64)
+        y, y_codes = {}, {}
+        for g in range(2):
+            y_codes[g] = keep.tile([P, D], U32, name="y_codes%d" % g, align_bytes=64)
+            for h in range(2):
+                y[g, h] = keep.tile([P, PACK, SPAN], F32, name="y%d%d" % (g, h))
+        x_words, x_grouped, w_raw, w_grouped, w_codes, w_scales, acc, y_grouped = {}, {}, {}, {}, {}, {}, {}, {}
+        whole, front, back = slice(0, SPAN), slice(0, HALF), slice(HALF, SPAN)
 
-        def load_x(s, ks=slice(0, K)):
+        def bank(i, shape):
+            return psum.tile(shape, F32, name="bank%d" % i, tag="bank%d" % i)
+
+        turned_banks = []
+
+        def turn_bank(shape, first=0):
+            turned_banks.append(first)
+            return bank(first + len(turned_banks) % (BANKS - first), shape)
+
+        def interleave(copy, dst, src):
+            copy(out=dst.rearrange("p (c i) t -> p c t i", i=4), in_=src.rearrange("p t (c i) -> p c t i", i=4))
+
+        def quantize(codes, scales, grouped):
+            nc.vector.quantize_mx(out=codes.bitcast(FP8X4), scales=scales, in_=grouped.rearrange("p c t -> p (c t)"))
+
+
+        def load_x(s, ks):
             g, t = divmod(s, PACK)
             width = ks.stop - ks.start
-            tile = raw.tile([P, width], BF16, name="x_raw", tag="x_raw", bufs=X_BUFS)
+            if s in CUT_STRIPS:
+                tile = raw.tile([P, width], BF16, name="x_cut", tag="x_cut", bufs=TURNS * len(CUT_STRIPS))
+            else:
+                tile = raw.tile([P, width], BF16, name="x_whole", tag="x_whole", bufs=WHOLE_STRIP_BUFS)
             src = patches[g * SPAN : (g + 1) * SPAN, ks].rearrange("(p t) k -> p t k", t=PACK)
             nc.sync.dma_start(out=tile[:], in_=src[:, t, :])
             for j in range(ks.start // SPAN, ks.stop // SPAN):
-                x_raw[s, j] = tile[:].bitcast(F32)[:, (j * SPAN - ks.start) // 2 : ((j + 1) * SPAN - ks.start) // 2]
+                first = (j * SPAN - ks.start) // 2
+                x_words[s, j] = tile[:].bitcast(F32)[:, first : first + SPAN // 2]
+
+        def load_x_turn(s, i):
+            load_x(s, slice(i * THIRD, (i + 1) * THIRD))
 
         def load_w(n):
             h, j = divmod(n, PASSES)
-            w_raw[n] = raw.tile([P, PACK, SPAN], BF16, name="w_raw", tag="w_raw", bufs=PASSES)
+            w_raw[n] = raw.tile([P, PACK, SPAN], BF16, name="w_raw", tag="w_raw")
             src = w_embed[j * SPAN : (j + 1) * SPAN, h * SPAN : (h + 1) * SPAN]
             nc.sync.dma_start(out=w_raw[n][:], in_=src.rearrange("(p t) d -> p t d", t=PACK))
 
@@ -86,276 +115,237 @@ def tile_patch_embed_token_planes_g2_kernel(tc, patches, w_embed, bias, row_pos,
             nc.sync.dma_start(out=tables[COL_END:ROW_END, :], in_=row_pos.rearrange("r (h d) -> (r h) d", h=2))
             nc.sync.dma_start(out=tables[ROW_END : ROW_END + 2, :], in_=bias.rearrange("(h d) -> h d", h=2))
 
+
         def turn_tables():
             words = tables[:].bitcast(F32)
-            turned = bank(next_bank(), [P, 2, P])
+            turned = turn_bank([P, 2, P])
             for b in range(2):
                 nc.tensor.transpose(turned[:, b, :], words[:, b * P : (b + 1) * P], ident[:])
-            nc.scalar.copy(out=rest_t[:], in_=turned[:, :, COL_END : ROW_END + 2])
-            nc.scalar.copy(out=cols_t[:], in_=turned[:, :, 0:COL_END].rearrange("n b (c u) -> n b u c", c=8))
+            nc.scalar.copy(out=rows_turned[:], in_=turned[:, :, COL_END : ROW_END + 2])
+            nc.scalar.copy(out=cols_turned[:], in_=turned[:, :, 0:COL_END].rearrange("n b (c u) -> n b u c", c=PER_ROW))
 
         def spread_tables():
-            for h in range(2):
-                rows = rest_t[:, :, h : 2 * GH : 2].unsqueeze(3).broadcast_to([P, 2, GH, P // GH])
-                nc.vector.tensor_copy(out=row_t[:, 2 * h : 2 * h + 2].rearrange("n b (r c) -> n b r c", r=GH), in_=rows)
+            values = rows_turned[:].bitcast(BF16)
+            rows = values[:, :, : 4 * GH].rearrange("n b (r v) -> n b r v", r=GH)
+            shift = values[:, :, 4 * GH :].unsqueeze(2).broadcast_to([P, 2, GH, 4])
+            nc.vector.tensor_tensor(out=row_bias[:], in0=rows, in1=shift, op=ADD)
             for b in range(2):
-                cols = cols_t[:, b].unsqueeze(2).broadcast_to([P, 8, GH, P // GH])
-                dst = col_t[:].rearrange("n t (h b) (r c) -> n b (t h) r c", b=2, r=GH)
-                nc.vector.tensor_copy(out=dst[:, b], in_=cols)
+                src = row_bias[:, b].rearrange("n r v -> n v r").unsqueeze(3).broadcast_to([P, 4, GH, PER_ROW])
+                nc.vector.tensor_copy(out=row_spread[:, b].rearrange("n v (r c) -> n v r c", r=GH), in_=src)
+            for b in range(2):
+                src = cols_turned[:, b].unsqueeze(2).broadcast_to([P, 2 * PACK, GH, PER_ROW])
+                dst = col_spread[:].rearrange("n t (h b) (r c) -> n b (t h) r c", b=2, r=GH)
+                nc.vector.tensor_copy(out=dst[:, b], in_=src)
 
-        def turn_bias():
-            turned = bank(next_bank(), [P, WORD_BLOCKS, P])
-            for h in range(2):
-                for b in range(2):
-                    column = rest_t[:, b, 2 * GH + h : 2 * GH + h + 1].to_broadcast([P, P])
-                    nc.tensor.transpose(turned[:, 2 * h + b, :], column, ident[:])
-            nc.scalar.copy(out=bias_all[:].bitcast(F32), in_=turned[:].rearrange("p b n -> p (b n)"))
+        def make_row_sum(h):
+            turned = turn_bank([P, 2, 2, P])
+            for b in range(2):
+                for e in range(2):
+                    nc.tensor.transpose(turned[:, b, e, :], row_spread[:, b, 2 * h + e, :], ident[:])
+            dst = row_sum[:, h * SPAN : (h + 1) * SPAN].rearrange("p (b n e) -> p b n e", b=2, e=2)
+            nc.scalar.copy(out=dst, in_=turned[:].rearrange("p b e n -> p b n e"))
 
-        def turn_rows():
-            turned = bank(next_bank(), [P, WORD_BLOCKS, P])
-            for b in range(WORD_BLOCKS):
-                nc.tensor.transpose(turned[:, b, :], row_t[:, b, :], ident[:])
-            return turned[:].rearrange("p b n -> p (b n)").bitcast(BF16)
-
-        def turn_cols(t):
-            turned = bank(next_bank(), [P, WORD_BLOCKS, P])
-            for b in range(WORD_BLOCKS):
-                nc.tensor.transpose(turned[:, b, :], col_t[:, t, b, :], ident[:])
-            return turned[:].rearrange("p b n -> p (b n)").bitcast(BF16)
-
-        def make_pos(t, col):
+        def make_pos(t):
+            turned = turn_bank([P, 4, P])
+            for hb in range(4):
+                nc.tensor.transpose(turned[:, hb, :], col_spread[:, t, hb, :], ident[:])
+            col = turned[:].rearrange("p hb n -> p (hb n)").bitcast(BF16)
             nc.vector.tensor_tensor(out=pos[:, t, :], in0=col, in1=row_sum[:], op=ADD)
 
-        banks_used = []
-        wide_rotation = [True]
 
-        def next_bank():
-            banks_used.append(0)
-            return len(banks_used) % 8 if wide_rotation else 4 + len(banks_used) % 4
-
-        def bank(i, shape):
-            return psum_acc.tile(shape, F32, name="bank%d" % i, tag="bank%d" % i)
-
-        def turn_x(b):
-            s, jj = divmod(b, PASSES // 2)
-            if b % 2 == 0:
-                x_grouped[b // 2] = stage.tile([P, SPAN, PACK], BF16, name="x_grouped", tag="x_grouped", align_bytes=64)
-            dst = x_grouped[b // 2][:].bitcast(F32).rearrange("p (b j r) u -> p b j r u", b=2, j=2)
-            xt = bank(next_bank(), [P, 2, 2, P])
+        def turn_x(i, first_bank):
+            s, jj = divmod(i, TURNS)
+            if i % 2 == 0:
+                x_grouped[i // 2] = stage.tile([P, SPAN, PACK], BF16, name="x_grouped", tag="x_grouped", align_bytes=64)
+            turned = turn_bank([P, 2, 2, P], first_bank)
             for j in range(2):
                 for u in range(2):
-                    nc.tensor.transpose(xt[:, j, u, :], x_raw[s, 2 * jj + j][:, u :: 2], ident[:])
-            copy = nc.vector.tensor_copy if b % VECTOR_EVERY == VECTOR_EVERY - 1 else nc.scalar.copy
-            copy(out=dst[:, b % 2], in_=xt[:].rearrange("p j u r -> p j r u"))
+                    nc.tensor.transpose(turned[:, j, u, :], x_words[s, 2 * jj + j][:, u::2], ident[:])
+            dst = x_grouped[i // 2][:].bitcast(F32).rearrange("p (i j r) u -> p i j r u", i=2, j=2)
+            nc.scalar.copy(out=dst[:, i % 2], in_=turned[:].rearrange("p j u r -> p j r u"))
 
-        def interleave(copy, dst, src):
-            copy(out=dst.rearrange("p (c i) t -> p c t i", i=4), in_=src.rearrange("p t (c i) -> p c t i", i=4))
+        def quantize_x(pair):
+            cols = slice(pair * SPAN, (pair + 1) * SPAN)
+            quantize(x_codes[:, cols], x_scales[:, cols], x_grouped[pair][:])
 
         def group_w(n):
-            split = W_VECTOR_COLS_HEAD if n < 2 else W_VECTOR_COLS_FIRST if n <= W_BEFORE_ADDS else W_VECTOR_COLS_SECOND
+            cut = VECTOR_COLS_EARLY if n < 2 else VECTOR_COLS_MIDDLE if n <= CHUNKS_BEFORE_ADDS else VECTOR_COLS_LATE
             w_grouped[n] = stage.tile([P, SPAN, PACK], BF16, name="w_grouped", tag="w_grouped", align_bytes=64)
-            interleave(nc.vector.tensor_copy, w_grouped[n][:, :split, :], w_raw[n][:, :, :split])
-            if split < SPAN:
-                interleave(nc.scalar.copy, w_grouped[n][:, split:, :], w_raw[n][:, :, split:])
-
-        def quantize(name, grouped):
-            codes = keep.tile([P, SPAN], U32, name=name + "_codes", align_bytes=64)
-            scales = keep.tile([P, SPAN], U8, name=name + "_scales", align_bytes=64)
-            nc.vector.quantize_mx(
-                out=codes[:].bitcast(FP8X4), scales=scales[:], in_=grouped[:].rearrange("p c t -> p (c t)")
-            )
-            return codes, scales
-
-        def quantize_x(n):
-            cols = slice(n * SPAN, (n + 1) * SPAN)
-            nc.vector.quantize_mx(
-                out=x_codes[:, cols].bitcast(FP8X4),
-                scales=x_scales[:, cols],
-                in_=x_grouped[n][:].rearrange("p c t -> p (c t)"),
-            )
+            interleave(nc.vector.tensor_copy, w_grouped[n][:, :cut, :], w_raw[n][:, :, :cut])
+            interleave(nc.scalar.copy, w_grouped[n][:, cut:, :], w_raw[n][:, :, cut:])
 
         def quantize_w(n):
-            w_codes[n], w_scales[n] = quantize("w%d" % n, w_grouped[n])
+            w_codes[n] = keep.tile([P, SPAN], U32, name="w%d_codes" % n, align_bytes=64)
+            w_scales[n] = keep.tile([P, SPAN], U8, name="w%d_scales" % n, align_bytes=64)
+            quantize(w_codes[n][:], w_scales[n][:], w_grouped[n][:])
+
 
         def multiply(dst, g, h, j, t, cols):
             first = ((g * PACK + t) * PASSES + j) * P
-            tok = slice(first, first + P)
             nc.tensor.matmul_mx(
                 out=dst,
-                lhsT=x_codes[:, tok].bitcast(FP8X4),
-                lhsT_scale=x_scales[:, tok],
+                lhsT=x_codes[:, first : first + P].bitcast(FP8X4),
+                lhsT_scale=x_scales[:, first : first + P],
                 rhs=w_codes[h * PASSES + j][:, cols].bitcast(FP8X4),
                 rhs_scale=w_scales[h * PASSES + j][:, cols],
                 start=(j == 0),
                 stop=(j == PASSES - 1),
             )
 
-        def multiply_pass(g, h, j, first_bank):
+        def multiply_pass(g, h, j):
             for t in range(PACK):
                 if j == 0:
-                    acc[g, h, t] = bank(first_bank + t, [P, SPAN])
+                    acc[g, h, t] = bank(PACK * g + t, [P, SPAN])
                 multiply(acc[g, h, t][:], g, h, j, t, whole)
 
-        def add_pos(g, h, t):
-            nc.vector.tensor_tensor(out=y[g, h][:, t, :], in0=acc[g, h, t][:], in1=pos[:, t, h * SPAN : (h + 1) * SPAN], op=ADD)
+        def finish_bank(g, h, t):
+            for j in range(PASS_MAJOR, PASSES):
+                multiply(acc[g, h, t][:], g, h, j, t, whole)
 
-        def store_y(g, h, cols, ts=slice(0, PACK)):
+        def multiply_last_unit(ts, cols, bank_index):
+            part = bank(bank_index, [P, ts.stop - ts.start, HALF])
+            for t in range(ts.start, ts.stop):
+                for j in range(PASSES):
+                    multiply(part[:, t - ts.start, :], 1, 1, j, t, cols)
+            return part
+
+
+        def add_pos(g, h, ts, cols, sums):
+            table = pos[:, ts, h * SPAN + cols.start : h * SPAN + cols.stop]
+            nc.vector.tensor_tensor(out=y[g, h][:, ts, cols], in0=sums, in1=table, op=ADD)
+
+        def add_bank(g, h, t):
+            add_pos(g, h, t, whole, acc[g, h, t][:])
+
+        def store_y(g, h, ts, cols):
             dst = out_0[g * SPAN : (g + 1) * SPAN, h * SPAN : (h + 1) * SPAN].rearrange("(p t) d -> p t d", t=PACK)
             nc.sync.dma_start(out=dst[:, ts, cols], in_=y[g, h][:, ts, cols])
 
         def group_y(g, h, cols, copy):
+            if cols.start == 0:
+                y_grouped[g, h] = stage.tile(
+                    [P, SPAN, PACK], BF16, name="y_grouped", tag="y_grouped", align_bytes=64, bufs=2
+                )
             interleave(copy, y_grouped[g, h][:, cols, :], y[g, h][:, :, cols])
 
         def quantize_y(g, h, cols):
-            wide = slice(h * SPAN + cols.start, h * SPAN + cols.stop)
-            nc.vector.quantize_mx(
-                out=y_codes[g][:, wide].bitcast(FP8X4),
-                scales=y_scales[4 * g :, wide],
-                in_=y_grouped[g, h][:, cols, :].rearrange("p c t -> p (c t)"),
-            )
+            features = slice(h * SPAN + cols.start, h * SPAN + cols.stop)
+            quantize(y_codes[g][:, features], y_scales[4 * g :, features], y_grouped[g, h][:, cols, :])
             dst = out_1[g].rearrange("p d t -> p (d t)").bitcast(I32)
-            nc.sync.dma_start(out=dst[:, wide], in_=y_codes[g][:, wide].bitcast(I32))
+            nc.sync.dma_start(out=dst[:, features], in_=y_codes[g][:, features].bitcast(I32))
 
-        whole = slice(0, SPAN)
-        y_grouped, y_codes = {}, {}
-        for g in range(2):
-            y_codes[g] = keep.tile([P, D], U32, name="y_codes%d" % g, align_bytes=64)
-            for h in range(2):
-                y[g, h] = keep.tile([P, PACK, SPAN], F32, name="y%d%d" % (g, h))
+        def store_scales(h, queues):
+            features = slice(h * SPAN, (h + 1) * SPAN)
+            for quad in range(4):
+                queues[quad % len(queues)].dma_start(
+                    out=out_2[:, 4 * quad : 4 * quad + 4, features].bitcast(I32),
+                    in_=y_scales[32 * quad : 32 * quad + 8, features].bitcast(I32),
+                )
 
-        def new_y_grouped(g, h):
-            y_grouped[g, h] = stage.tile([P, SPAN, PACK], BF16, name="y_grouped", tag="y_grouped", align_bytes=64, bufs=2)
 
-        def piece(g, c, ts, bank_index):
-            cols = slice(c * HALF, (c + 1) * HALF)
-            part = bank(bank_index, [P, ts.stop - ts.start, HALF])
-            for t in range(ts.start, ts.stop):
-                for j in range(PASSES):
-                    multiply(part[:, t - ts.start, :], g, 1, j, t, cols)
-            return part
-
-        def add_piece(g, c, ts, part):
-            cols = slice(c * HALF, (c + 1) * HALF)
-            nc.vector.tensor_tensor(out=y[g, 1][:, ts, cols], in0=part[:], in1=pos[:, ts, SPAN + c * HALF : SPAN + (c + 1) * HALF], op=ADD)
-
-        low, high = slice(0, 2), slice(2, 4)
+        load_x_turn(0, 0)
         load_tables()
         make_identity(nc, ident[:])
-        load_x(0, slice(0, K // 3))
-        load_x(0, slice(K // 3, K))
-        for s in range(1, X_BUFS - 1):
-            load_x(s)
+        for i in range(1, TURNS):
+            load_x_turn(0, i)
+        for s in range(1, WHOLE_STRIP_BUFS + 1):
+            load_x(s, slice(0, K))
 
         turn_tables()
         spread_tables()
-        turn_bias()
-        for b in range(X_BANKS):
-            if b == 3:
-                load_x(5)
-                load_w(0)
-                load_x(6)
-                load_w(1)
-            if b == 6:
-                load_x(7)
-                for m in range(2, PASSES):
-                    load_w(m)
-            if b == 1:
-                rows = turn_rows()
-                nc.vector.tensor_tensor(out=row_sum[:], in0=rows, in1=bias_all[:], op=ADD)
-            if b == 17:
-                wide_rotation.clear()
-            for t in range(PACK):
-                if COL_AT[t] == b:
-                    make_pos(t, turn_cols(t))
-            if b == W0_AT:
-                group_w(0)
-            if b == W1_AT:
-                group_w(1)
-            if b == 21:
-                multiply_pass(0, 0, 0, 0)
-            turn_x(b)
-            if b == W0_AT + 1:
-                quantize_w(0)
-            if b == W1_AT + 1:
-                quantize_w(1)
-            if b % 2 == 0 and b > 0:
-                quantize_x(b // 2 - 1)
-        group_w(2)
-        quantize_x(X_BANKS // 2 - 1)
-        for m in range(2, W_BEFORE_ADDS):
-            if m == 2:
-                load_w(PASSES)
-            if m < PASSES:
-                load_w(PASSES + m - 1)
-            if m == PASSES - 1:
-                load_w(CHUNKS - 1)
-            group_w(m + 1)
-            quantize_w(m)
-        multiply_pass(0, 0, 1, 0)
-        multiply_pass(1, 0, 0, 4)
-        multiply_pass(1, 0, 1, 4)
-        for j in range(2, PASS_MAJOR_FIRST):
-            for g in range(2):
-                multiply_pass(g, 0, j, 4 * g)
-        for s in range(STRIPS):
-            g, t = divmod(s, PACK)
-            for j in range(PASS_MAJOR_FIRST, PASSES):
-                multiply(acc[g, 0, t][:], g, 0, j, t, whole)
-        for t in range(PACK):
-            add_pos(0, 0, t)
-        store_y(0, 0, whole)
-        done = 0
-        for m in range(W_BEFORE_ADDS, CHUNKS):
-            if m + 1 < CHUNKS:
-                group_w(m + 1)
-            else:
-                add_pos(1, 0, 0)
-                done = 1
-            quantize_w(m)
-        for t in range(done, PACK):
-            add_pos(1, 0, t)
-        store_y(1, 0, whole)
+        for i in range(STRIPS * TURNS):
+            s, jj = divmod(i, TURNS)
+            early_chunk = s - (STRIPS - 3)
+            if jj == 0:
+                if s == 1:
+                    make_row_sum(0)
+                    make_row_sum(1)
+                if s == 2:
+                    load_x(STRIPS - 3, slice(0, K))
+                    for n in range(2):
+                        load_w(n)
+                        for k_part in range(TURNS):
+                            load_x_turn(STRIPS - 2 + n, k_part)
+                    for n in range(2, PASSES):
+                        load_w(n)
+                if 1 <= s <= PACK:
+                    make_pos(s - 1)
+                if early_chunk in (0, 1):
+                    group_w(early_chunk)
+                if s == STRIPS - 1:
+                    multiply_pass(0, 0, 0)
+            turn_x(i, PACK if s >= STRIPS - 2 else 0)
+            if jj == 1 and early_chunk in (0, 1):
+                quantize_w(early_chunk)
+            if i % 2 == 0 and i > 0:
+                quantize_x(i // 2 - 1)
 
-        halves = [slice(0, HALF), slice(HALF, SPAN)]
-        new_y_grouped(0, 0)
+
+        group_w(2)
+        quantize_x(STRIPS * TURNS // 2 - 1)
+        load_w(PASSES)
+        for n in range(2, CHUNKS_BEFORE_ADDS):
+            if n < PASSES:
+                load_w(PASSES + n - 1)
+            if n == PASSES - 1:
+                load_w(CHUNKS - 1)
+            group_w(n + 1)
+            quantize_w(n)
+        multiply_pass(0, 0, 1)
+        multiply_pass(1, 0, 0)
+        multiply_pass(1, 0, 1)
+        for j in range(2, PASS_MAJOR):
+            for g in range(2):
+                multiply_pass(g, 0, j)
+        for g in range(2):
+            for t in range(PACK):
+                finish_bank(g, 0, t)
+        for t in range(PACK):
+            add_bank(0, 0, t)
+        store_y(0, 0, slice(0, PACK), whole)
+        for n in range(CHUNKS_BEFORE_ADDS, CHUNKS - 1):
+            group_w(n + 1)
+            quantize_w(n)
+        for t in range(PACK):
+            add_bank(1, 0, t)
+            if t == 0:
+                quantize_w(CHUNKS - 1)
+            if t % 2 == 1:
+                store_y(1, 0, slice(t - 1, t + 1), whole)
+
+
         group_y(0, 0, whole, nc.scalar.copy)
-        new_y_grouped(1, 0)
         group_y(1, 0, whole, nc.scalar.copy)
         for j in range(PASS_MAJOR):
-            multiply_pass(0, 1, j, 0)
+            multiply_pass(0, 1, j)
         for t in range(PACK):
-            for j in range(PASS_MAJOR, PASSES):
-                multiply(acc[0, 1, t][:], 0, 1, j, t, whole)
-            add_pos(0, 1, t)
-            store_y(0, 1, whole, slice(t, t + 1))
-            if t == 1:
+            finish_bank(0, 1, t)
+            add_bank(0, 1, t)
+            store_y(0, 1, slice(t, t + 1), whole)
+            if t == 0:
                 quantize_y(0, 0, whole)
         quantize_y(1, 0, whole)
-        new_y_grouped(0, 1)
+        store_scales(0, [nc.sync])
         group_y(0, 1, whole, nc.scalar.copy)
 
-        parts = [piece(1, 0, low, 4), piece(1, 0, high, 5)]
-        add_piece(1, 0, low, parts[0])
-        add_piece(1, 0, high, parts[1])
-        store_y(1, 1, halves[0])
-        new_y_grouped(1, 1)
-        group_y(1, 1, halves[0], nc.scalar.copy)
+
+        pairs = [slice(0, 2), slice(2, 4)]
+        sums = [multiply_last_unit(ts, front, PACK + i) for i, ts in enumerate(pairs)]
+        for ts, part in zip(pairs, sums):
+            add_pos(1, 1, ts, front, part[:])
+        store_y(1, 1, slice(0, PACK), front)
+        group_y(1, 1, front, nc.scalar.copy)
         quantize_y(0, 1, whole)
 
         for t in range(PACK):
             one = slice(t, t + 1)
-            add_piece(1, 1, one, piece(1, 1, one, (6 + t) % 8))
+            add_pos(1, 1, one, back, multiply_last_unit(one, back, (PACK + 2 + t) % BANKS)[:])
             if t == 2:
-                quantize_y(1, 1, halves[0])
+                quantize_y(1, 1, front)
             if t % 2 == 1:
-                store_y(1, 1, halves[1], slice(t - 1, t + 1))
-        cut = HALF + TAIL_VECTOR_COLS
+                store_y(1, 1, slice(t - 1, t + 1), back)
+        cut = HALF + VECTOR_COLS_LAST
         group_y(1, 1, slice(HALF, cut), nc.vector.tensor_copy)
         group_y(1, 1, slice(cut, SPAN), nc.scalar.copy)
-        quantize_y(1, 1, halves[1])
-        scale_rows = out_2.bitcast(I32)
-        for q in range(4):
-            queue = nc.sync if q % 2 == 0 else nc.scalar
-            queue.dma_start(
-                out=scale_rows[:, 4 * q : 4 * q + 4, :], in_=y_scales[32 * q : 32 * q + 8, :].bitcast(I32)
-            )
+        quantize_y(1, 1, back)
+        store_scales(1, [nc.sync, nc.scalar])

@@ -25,19 +25,22 @@ BANKS = 8
 
 TURNS = PASSES // 2
 THIRD = K // TURNS
-WHOLE_STRIP_BUFS = 4
-CUT_STRIPS = (0, STRIPS - 2, STRIPS - 1)
+X_TILES = 6
+W0_TURN = 5 * TURNS + 1
+W1_TURN = 7 * TURNS
+FIRST_PRODUCT_TURN = 7 * TURNS
+RUN = 2
 
 COL_END = 2 * GW
 ROW_END = COL_END + 2 * GH
 PER_ROW = P // GH
 
 VECTOR_COLS_EARLY = 384
-VECTOR_COLS_MIDDLE = 256
+VECTOR_COLS_MIDDLE = SPAN // 2
 VECTOR_COLS_LATE = 192
 VECTOR_COLS_LAST = 160
 CHUNKS_BEFORE_ADDS = 8
-PASS_MAJOR = 4
+PASS_MAJOR = (4, PASSES // 2)
 
 
 def tile_patch_embed_token_planes_g2_kernel(
@@ -53,11 +56,11 @@ def tile_patch_embed_token_planes_g2_kernel(
 
         ident = keep.tile([P, P], F32, name="ident")
         tables = keep.tile([P, SPAN], BF16, name="tables")
-        rows_turned = keep.tile([P, 2, 2 * GH + 2], F32, name="rows_turned")
-        cols_turned = keep.tile([P, 2, 2 * PACK, PER_ROW], F32, name="cols_turned")
-        row_bias = keep.tile([P, 2, GH, 4], F32, name="row_bias")
-        row_spread = keep.tile([P, 2, 4, P], F32, name="row_spread")
-        col_spread = keep.tile([P, PACK, 4, P], F32, name="col_spread")
+        rest_t = keep.tile([P, 2, 2 * GH + 2], F32, name="rest_t")
+        cols_t = keep.tile([P, 2, 2 * PACK, PER_ROW], F32, name="cols_t")
+        row_t = keep.tile([P, 4, P], F32, name="row_t")
+        col_t = keep.tile([P, PACK, 4, P], F32, name="col_t")
+        bias_all = keep.tile([P, D], BF16, name="bias_all")
         row_sum = keep.tile([P, D], F32, name="row_sum")
         pos = keep.tile([P, PACK, D], F32, name="pos")
         x_codes = keep.tile([P, STRIPS * PASSES * P], U32, name="x_codes", align_bytes=64)
@@ -81,31 +84,24 @@ def tile_patch_embed_token_planes_g2_kernel(
             return bank(first + len(turned_banks) % (BANKS - first), shape)
 
         def interleave(copy, dst, src):
-            copy(out=dst.rearrange("p (c i) t -> p c t i", i=4), in_=src.rearrange("p t (c i) -> p c t i", i=4))
+            copy(out=dst.rearrange("p (c i) t -> p c t i", i=RUN), in_=src.rearrange("p t (c i) -> p c t i", i=RUN))
 
         def quantize(codes, scales, grouped):
             nc.vector.quantize_mx(out=codes.bitcast(FP8X4), scales=scales, in_=grouped.rearrange("p c t -> p (c t)"))
 
 
-        def load_x(s, ks):
+        def load_x(s, ks=slice(0, K)):
             g, t = divmod(s, PACK)
-            width = ks.stop - ks.start
-            if s in CUT_STRIPS:
-                tile = raw.tile([P, width], BF16, name="x_cut", tag="x_cut", bufs=TURNS * len(CUT_STRIPS))
-            else:
-                tile = raw.tile([P, width], BF16, name="x_whole", tag="x_whole", bufs=WHOLE_STRIP_BUFS)
+            tile = raw.tile([P, ks.stop - ks.start], BF16, name="x_raw", tag="x_raw", bufs=X_TILES)
             src = patches[g * SPAN : (g + 1) * SPAN, ks].rearrange("(p t) k -> p t k", t=PACK)
             nc.sync.dma_start(out=tile[:], in_=src[:, t, :])
             for j in range(ks.start // SPAN, ks.stop // SPAN):
                 first = (j * SPAN - ks.start) // 2
                 x_words[s, j] = tile[:].bitcast(F32)[:, first : first + SPAN // 2]
 
-        def load_x_turn(s, i):
-            load_x(s, slice(i * THIRD, (i + 1) * THIRD))
-
         def load_w(n):
             h, j = divmod(n, PASSES)
-            w_raw[n] = raw.tile([P, PACK, SPAN], BF16, name="w_raw", tag="w_raw")
+            w_raw[n] = raw.tile([P, PACK, SPAN], BF16, name="w_raw", tag="w_raw", bufs=PASSES)
             src = w_embed[j * SPAN : (j + 1) * SPAN, h * SPAN : (h + 1) * SPAN]
             nc.sync.dma_start(out=w_raw[n][:], in_=src.rearrange("(p t) d -> p t d", t=PACK))
 
@@ -121,34 +117,37 @@ def tile_patch_embed_token_planes_g2_kernel(
             turned = turn_bank([P, 2, P])
             for b in range(2):
                 nc.tensor.transpose(turned[:, b, :], words[:, b * P : (b + 1) * P], ident[:])
-            nc.scalar.copy(out=rows_turned[:], in_=turned[:, :, COL_END : ROW_END + 2])
-            nc.scalar.copy(out=cols_turned[:], in_=turned[:, :, 0:COL_END].rearrange("n b (c u) -> n b u c", c=PER_ROW))
+            nc.scalar.copy(out=rest_t[:], in_=turned[:, :, COL_END : ROW_END + 2])
+            nc.scalar.copy(out=cols_t[:], in_=turned[:, :, 0:COL_END].rearrange("n b (c u) -> n b u c", c=PER_ROW))
 
         def spread_tables():
-            values = rows_turned[:].bitcast(BF16)
-            rows = values[:, :, : 4 * GH].rearrange("n b (r v) -> n b r v", r=GH)
-            shift = values[:, :, 4 * GH :].unsqueeze(2).broadcast_to([P, 2, GH, 4])
-            nc.vector.tensor_tensor(out=row_bias[:], in0=rows, in1=shift, op=ADD)
+            for h in range(2):
+                src = rest_t[:, :, h : 2 * GH : 2].unsqueeze(3).broadcast_to([P, 2, GH, PER_ROW])
+                nc.vector.tensor_copy(out=row_t[:, 2 * h : 2 * h + 2].rearrange("n b (r c) -> n b r c", r=GH), in_=src)
             for b in range(2):
-                src = row_bias[:, b].rearrange("n r v -> n v r").unsqueeze(3).broadcast_to([P, 4, GH, PER_ROW])
-                nc.vector.tensor_copy(out=row_spread[:, b].rearrange("n v (r c) -> n v r c", r=GH), in_=src)
-            for b in range(2):
-                src = cols_turned[:, b].unsqueeze(2).broadcast_to([P, 2 * PACK, GH, PER_ROW])
-                dst = col_spread[:].rearrange("n t (h b) (r c) -> n b (t h) r c", b=2, r=GH)
+                src = cols_t[:, b].unsqueeze(2).broadcast_to([P, 2 * PACK, GH, PER_ROW])
+                dst = col_t[:].rearrange("n t (h b) (r c) -> n b (t h) r c", b=2, r=GH)
                 nc.vector.tensor_copy(out=dst[:, b], in_=src)
 
-        def make_row_sum(h):
-            turned = turn_bank([P, 2, 2, P])
-            for b in range(2):
-                for e in range(2):
-                    nc.tensor.transpose(turned[:, b, e, :], row_spread[:, b, 2 * h + e, :], ident[:])
-            dst = row_sum[:, h * SPAN : (h + 1) * SPAN].rearrange("p (b n e) -> p b n e", b=2, e=2)
-            nc.scalar.copy(out=dst, in_=turned[:].rearrange("p b e n -> p b n e"))
+        def make_bias_all():
+            turned = turn_bank([P, 4, P])
+            for h in range(2):
+                for b in range(2):
+                    column = rest_t[:, b, 2 * GH + h : 2 * GH + h + 1].to_broadcast([P, P])
+                    nc.tensor.transpose(turned[:, 2 * h + b, :], column, ident[:])
+            nc.scalar.copy(out=bias_all[:].bitcast(F32), in_=turned[:].rearrange("p hb n -> p (hb n)"))
+
+        def make_row_sum():
+            turned = turn_bank([P, 4, P])
+            for hb in range(4):
+                nc.tensor.transpose(turned[:, hb, :], row_t[:, hb, :], ident[:])
+            row = turned[:].rearrange("p hb n -> p (hb n)").bitcast(BF16)
+            nc.vector.tensor_tensor(out=row_sum[:], in0=row, in1=bias_all[:], op=ADD)
 
         def make_pos(t):
             turned = turn_bank([P, 4, P])
             for hb in range(4):
-                nc.tensor.transpose(turned[:, hb, :], col_spread[:, t, hb, :], ident[:])
+                nc.tensor.transpose(turned[:, hb, :], col_t[:, t, hb, :], ident[:])
             col = turned[:].rearrange("p hb n -> p (hb n)").bitcast(BF16)
             nc.vector.tensor_tensor(out=pos[:, t, :], in0=col, in1=row_sum[:], op=ADD)
 
@@ -199,7 +198,7 @@ def tile_patch_embed_token_planes_g2_kernel(
                 multiply(acc[g, h, t][:], g, h, j, t, whole)
 
         def finish_bank(g, h, t):
-            for j in range(PASS_MAJOR, PASSES):
+            for j in range(PASS_MAJOR[h], PASSES):
                 multiply(acc[g, h, t][:], g, h, j, t, whole)
 
         def multiply_last_unit(ts, cols, bank_index):
@@ -234,49 +233,42 @@ def tile_patch_embed_token_planes_g2_kernel(
             dst = out_1[g].rearrange("p d t -> p (d t)").bitcast(I32)
             nc.sync.dma_start(out=dst[:, features], in_=y_codes[g][:, features].bitcast(I32))
 
-        def store_scales(h, queues):
-            features = slice(h * SPAN, (h + 1) * SPAN)
-            for quad in range(4):
-                queues[quad % len(queues)].dma_start(
-                    out=out_2[:, 4 * quad : 4 * quad + 4, features].bitcast(I32),
-                    in_=y_scales[32 * quad : 32 * quad + 8, features].bitcast(I32),
-                )
 
-
-        load_x_turn(0, 0)
         load_tables()
         make_identity(nc, ident[:])
-        for i in range(1, TURNS):
-            load_x_turn(0, i)
-        for s in range(1, WHOLE_STRIP_BUFS + 1):
-            load_x(s, slice(0, K))
+        load_x(0, slice(0, THIRD))
+        load_x(0, slice(THIRD, K))
+        for s in range(1, X_TILES - 1):
+            load_x(s)
 
         turn_tables()
         spread_tables()
+        make_bias_all()
         for i in range(STRIPS * TURNS):
             s, jj = divmod(i, TURNS)
-            early_chunk = s - (STRIPS - 3)
-            if jj == 0:
-                if s == 1:
-                    make_row_sum(0)
-                    make_row_sum(1)
-                if s == 2:
-                    load_x(STRIPS - 3, slice(0, K))
-                    for n in range(2):
-                        load_w(n)
-                        for k_part in range(TURNS):
-                            load_x_turn(STRIPS - 2 + n, k_part)
-                    for n in range(2, PASSES):
-                        load_w(n)
-                if 1 <= s <= PACK:
-                    make_pos(s - 1)
-                if early_chunk in (0, 1):
-                    group_w(early_chunk)
-                if s == STRIPS - 1:
-                    multiply_pass(0, 0, 0)
-            turn_x(i, PACK if s >= STRIPS - 2 else 0)
-            if jj == 1 and early_chunk in (0, 1):
-                quantize_w(early_chunk)
+            if i == TURNS:
+                for n in range(2):
+                    load_x(X_TILES - 1 + n)
+                    load_w(n)
+            if i == 2 * TURNS:
+                load_x(STRIPS - 1)
+                for n in range(2, PASSES):
+                    load_w(n)
+            if i == 1:
+                make_row_sum()
+            if jj == 0 and 1 <= s <= PACK:
+                make_pos(s - 1)
+            if i == W0_TURN:
+                group_w(0)
+            if i == W1_TURN:
+                group_w(1)
+            if i == FIRST_PRODUCT_TURN:
+                multiply_pass(0, 0, 0)
+            turn_x(i, PACK if i >= FIRST_PRODUCT_TURN - PACK else 0)
+            if i == W0_TURN + 1:
+                quantize_w(0)
+            if i == W1_TURN + 1:
+                quantize_w(1)
             if i % 2 == 0 and i > 0:
                 quantize_x(i // 2 - 1)
 
@@ -294,7 +286,7 @@ def tile_patch_embed_token_planes_g2_kernel(
         multiply_pass(0, 0, 1)
         multiply_pass(1, 0, 0)
         multiply_pass(1, 0, 1)
-        for j in range(2, PASS_MAJOR):
+        for j in range(2, PASS_MAJOR[0]):
             for g in range(2):
                 multiply_pass(g, 0, j)
         for g in range(2):
@@ -310,22 +302,20 @@ def tile_patch_embed_token_planes_g2_kernel(
             add_bank(1, 0, t)
             if t == 0:
                 quantize_w(CHUNKS - 1)
-            if t % 2 == 1:
-                store_y(1, 0, slice(t - 1, t + 1), whole)
+        store_y(1, 0, slice(0, PACK), whole)
 
 
         group_y(0, 0, whole, nc.scalar.copy)
         group_y(1, 0, whole, nc.scalar.copy)
-        for j in range(PASS_MAJOR):
+        for j in range(PASS_MAJOR[1]):
             multiply_pass(0, 1, j)
         for t in range(PACK):
             finish_bank(0, 1, t)
             add_bank(0, 1, t)
             store_y(0, 1, slice(t, t + 1), whole)
-            if t == 0:
+            if t == 1:
                 quantize_y(0, 0, whole)
         quantize_y(1, 0, whole)
-        store_scales(0, [nc.sync])
         group_y(0, 1, whole, nc.scalar.copy)
 
 
@@ -348,4 +338,10 @@ def tile_patch_embed_token_planes_g2_kernel(
         group_y(1, 1, slice(HALF, cut), nc.vector.tensor_copy)
         group_y(1, 1, slice(cut, SPAN), nc.scalar.copy)
         quantize_y(1, 1, back)
-        store_scales(1, [nc.sync, nc.scalar])
+        scale_rows = out_2.bitcast(I32)
+        for quad in range(4):
+            queue = nc.sync if quad % 2 == 0 else nc.scalar
+            queue.dma_start(
+                out=scale_rows[:, 4 * quad : 4 * quad + 4, :],
+                in_=y_scales[32 * quad : 32 * quad + 8, :].bitcast(I32),
+            )

from contextlib import ExitStack

import concourse.mybir as mybir
from concourse.masks import make_identity

GH, GW, T, K, D = 16, 32, 1024, 3072, 1024
FLOPS = 2 * T * K * D

F32 = mybir.dt.float32
BF16 = mybir.dt.bfloat16
I32 = mybir.dt.int32
U32 = mybir.dt.uint32
U8 = mybir.dt.uint8
FP8X4 = mybir.dt.float8_e4m3fn_x4
ADD = mybir.AluOpType.add

P = 128
PACK = 4
SPAN = P * PACK
HALF = SPAN // 2
PASSES = K // SPAN
CHUNKS = 2 * PASSES
STRIPS = 2 * PACK
BANKS = 8

TURNS = PASSES // 2
THIRD = K // TURNS
X_TILES = 6
W0_TURN = 5 * TURNS + 1
W1_TURN = 7 * TURNS
FIRST_PRODUCT_TURN = 7 * TURNS
RUN = 2

COL_END = 2 * GW
ROW_END = COL_END + 2 * GH
PER_ROW = P // GH

VECTOR_COLS_EARLY = 384
VECTOR_COLS_MIDDLE = SPAN // 2
VECTOR_COLS_LATE = 192
VECTOR_COLS_LAST = 160
CHUNKS_BEFORE_ADDS = 8
PASS_MAJOR = (4, PASSES // 2)


def tile_patch_embed_token_planes_g2_kernel(
    tc, patches, w_embed, bias, row_pos, col_pos, out_0, out_1, out_2
):
    nc = tc.nc
    with ExitStack() as ctx:
        keep = ctx.enter_context(tc.tile_pool(name="keep", bufs=1))
        raw = ctx.enter_context(tc.tile_pool(name="raw", bufs=PASSES))
        stage = ctx.enter_context(tc.tile_pool(name="stage", bufs=3))
        psum = ctx.enter_context(tc.psum_pool(name="psum", bufs=1))
        ctx.enter_context(tc.manual_schedule())

        ident = keep.tile([P, P], F32, name="ident")
        tables = keep.tile([P, SPAN], BF16, name="tables")
        rest_t = keep.tile([P, 2, 2 * GH + 2], F32, name="rest_t")
        cols_t = keep.tile([P, 2, 2 * PACK, PER_ROW], F32, name="cols_t")
        row_t = keep.tile([P, 4, P], F32, name="row_t")
        col_t = keep.tile([P, PACK, 4, P], F32, name="col_t")
        bias_all = keep.tile([P, D], BF16, name="bias_all")
        row_sum = keep.tile([P, D], F32, name="row_sum")
        pos = keep.tile([P, PACK, D], F32, name="pos")
        x_codes = keep.tile([P, STRIPS * PASSES * P], U32, name="x_codes", align_bytes=64)
        x_scales = keep.tile([P, STRIPS * PASSES * P], U8, name="x_scales", align_bytes=64)
        y_scales = keep.tile([P, D], U8, name="y_scales", align_bytes=64)
        y, y_codes = {}, {}
        for g in range(2):
            y_codes[g] = keep.tile([P, D], U32, name="y_codes%d" % g, align_bytes=64)
            for h in range(2):
                y[g, h] = keep.tile([P, PACK, SPAN], F32, name="y%d%d" % (g, h))
        x_words, x_grouped, w_raw, w_grouped, w_codes, w_scales, acc, y_grouped = {}, {}, {}, {}, {}, {}, {}, {}
        whole, front, back = slice(0, SPAN), slice(0, HALF), slice(HALF, SPAN)

        def bank(i, shape):
            return psum.tile(shape, F32, name="bank%d" % i, tag="bank%d" % i)

        turned_banks = []

        def turn_bank(shape, first=0):
            turned_banks.append(first)
            return bank(first + len(turned_banks) % (BANKS - first), shape)

        def interleave(copy, dst, src):
            copy(out=dst.rearrange("p (c i) t -> p c t i", i=RUN), in_=src.rearrange("p t (c i) -> p c t i", i=RUN))

        def quantize(codes, scales, grouped):
            nc.vector.quantize_mx(out=codes.bitcast(FP8X4), scales=scales, in_=grouped.rearrange("p c t -> p (c t)"))


        def load_x(s, ks=slice(0, K)):
            g, t = divmod(s, PACK)
            tile = raw.tile([P, ks.stop - ks.start], BF16, name="x_raw", tag="x_raw", bufs=X_TILES)
            src = patches[g * SPAN : (g + 1) * SPAN, ks].rearrange("(p t) k -> p t k", t=PACK)
            nc.sync.dma_start(out=tile[:], in_=src[:, t, :])
            for j in range(ks.start // SPAN, ks.stop // SPAN):
                first = (j * SPAN - ks.start) // 2
                x_words[s, j] = tile[:].bitcast(F32)[:, first : first + SPAN // 2]

        def load_w(n):
            h, j = divmod(n, PASSES)
            w_raw[n] = raw.tile([P, PACK, SPAN], BF16, name="w_raw", tag="w_raw", bufs=PASSES)
            src = w_embed[j * SPAN : (j + 1) * SPAN, h * SPAN : (h + 1) * SPAN]
            nc.sync.dma_start(out=w_raw[n][:], in_=src.rearrange("(p t) d -> p t d", t=PACK))

        def load_tables():
            nc.gpsimd.memset(tables[ROW_END:P, :].bitcast(I32), 0)
            nc.sync.dma_start(out=tables[0:COL_END, :], in_=col_pos.rearrange("c (h d) -> (c h) d", h=2))
            nc.sync.dma_start(out=tables[COL_END:ROW_END, :], in_=row_pos.rearrange("r (h d) -> (r h) d", h=2))
            nc.sync.dma_start(out=tables[ROW_END : ROW_END + 2, :], in_=bias.rearrange("(h d) -> h d", h=2))


        def turn_tables():
            words = tables[:].bitcast(F32)
            turned = turn_bank([P, 2, P])
            for b in range(2):
                nc.tensor.transpose(turned[:, b, :], words[:, b * P : (b + 1) * P], ident[:])
            nc.scalar.copy(out=rest_t[:], in_=turned[:, :, COL_END : ROW_END + 2])
            nc.scalar.copy(out=cols_t[:], in_=turned[:, :, 0:COL_END].rearrange("n b (c u) -> n b u c", c=PER_ROW))

        def spread_tables():
            for h in range(2):
                src = rest_t[:, :, h : 2 * GH : 2].unsqueeze(3).broadcast_to([P, 2, GH, PER_ROW])
                nc.vector.tensor_copy(out=row_t[:, 2 * h : 2 * h + 2].rearrange("n b (r c) -> n b r c", r=GH), in_=src)
            for b in range(2):
                src = cols_t[:, b].unsqueeze(2).broadcast_to([P, 2 * PACK, GH, PER_ROW])
                dst = col_t[:].rearrange("n t (h b) (r c) -> n b (t h) r c", b=2, r=GH)
                nc.vector.tensor_copy(out=dst[:, b], in_=src)

        def make_bias_all():
            turned = turn_bank([P, 4, P])
            for h in range(2):
                for b in range(2):
                    column = rest_t[:, b, 2 * GH + h : 2 * GH + h + 1].to_broadcast([P, P])
                    nc.tensor.transpose(turned[:, 2 * h + b, :], column, ident[:])
            nc.scalar.copy(out=bias_all[:].bitcast(F32), in_=turned[:].rearrange("p hb n -> p (hb n)"))

        def make_row_sum():
            turned = turn_bank([P, 4, P])
            for hb in range(4):
                nc.tensor.transpose(turned[:, hb, :], row_t[:, hb, :], ident[:])
            row = turned[:].rearrange("p hb n -> p (hb n)").bitcast(BF16)
            nc.vector.tensor_tensor(out=row_sum[:], in0=row, in1=bias_all[:], op=ADD)

        def make_pos(t):
            turned = turn_bank([P, 4, P])
            for hb in range(4):
                nc.tensor.transpose(turned[:, hb, :], col_t[:, t, hb, :], ident[:])
            col = turned[:].rearrange("p hb n -> p (hb n)").bitcast(BF16)
            nc.vector.tensor_tensor(out=pos[:, t, :], in0=col, in1=row_sum[:], op=ADD)


        def turn_x(i, first_bank):
            s, jj = divmod(i, TURNS)
            if i % 2 == 0:
                x_grouped[i // 2] = stage.tile([P, SPAN, PACK], BF16, name="x_grouped", tag="x_grouped", align_bytes=64)
            turned = turn_bank([P, 2, 2, P], first_bank)
            for j in range(2):
                for u in range(2):
                    nc.tensor.transpose(turned[:, j, u, :], x_words[s, 2 * jj + j][:, u::2], ident[:])
            dst = x_grouped[i // 2][:].bitcast(F32).rearrange("p (i j r) u -> p i j r u", i=2, j=2)
            nc.scalar.copy(out=dst[:, i % 2], in_=turned[:].rearrange("p j u r -> p j r u"))

        def quantize_x(pair):
            cols = slice(pair * SPAN, (pair + 1) * SPAN)
            quantize(x_codes[:, cols], x_scales[:, cols], x_grouped[pair][:])

        def group_w(n):
            cut = VECTOR_COLS_EARLY if n < 2 else VECTOR_COLS_MIDDLE if n <= CHUNKS_BEFORE_ADDS else VECTOR_COLS_LATE
            w_grouped[n] = stage.tile([P, SPAN, PACK], BF16, name="w_grouped", tag="w_grouped", align_bytes=64)
            interleave(nc.vector.tensor_copy, w_grouped[n][:, :cut, :], w_raw[n][:, :, :cut])
            interleave(nc.scalar.copy, w_grouped[n][:, cut:, :], w_raw[n][:, :, cut:])

        def quantize_w(n):
            w_codes[n] = keep.tile([P, SPAN], U32, name="w%d_codes" % n, align_bytes=64)
            w_scales[n] = keep.tile([P, SPAN], U8, name="w%d_scales" % n, align_bytes=64)
            quantize(w_codes[n][:], w_scales[n][:], w_grouped[n][:])


        def multiply(dst, g, h, j, t, cols):
            first = ((g * PACK + t) * PASSES + j) * P
            nc.tensor.matmul_mx(
                out=dst,
                lhsT=x_codes[:, first : first + P].bitcast(FP8X4),
                lhsT_scale=x_scales[:, first : first + P],
                rhs=w_codes[h * PASSES + j][:, cols].bitcast(FP8X4),
                rhs_scale=w_scales[h * PASSES + j][:, cols],
                start=(j == 0),
                stop=(j == PASSES - 1),
            )

        def multiply_pass(g, h, j):
            for t in range(PACK):
                if j == 0:
                    acc[g, h, t] = bank(PACK * g + t, [P, SPAN])
                multiply(acc[g, h, t][:], g, h, j, t, whole)

        def finish_bank(g, h, t):
            for j in range(PASS_MAJOR[h], PASSES):
                multiply(acc[g, h, t][:], g, h, j, t, whole)

        def multiply_last_unit(ts, cols, bank_index):
            part = bank(bank_index, [P, ts.stop - ts.start, HALF])
            for t in range(ts.start, ts.stop):
                for j in range(PASSES):
                    multiply(part[:, t - ts.start, :], 1, 1, j, t, cols)
            return part


        def add_pos(g, h, ts, cols, sums):
            table = pos[:, ts, h * SPAN + cols.start : h * SPAN + cols.stop]
            nc.vector.tensor_tensor(out=y[g, h][:, ts, cols], in0=sums, in1=table, op=ADD)

        def add_bank(g, h, t):
            add_pos(g, h, t, whole, acc[g, h, t][:])

        def store_y(g, h, ts, cols):
            dst = out_0[g * SPAN : (g + 1) * SPAN, h * SPAN : (h + 1) * SPAN].rearrange("(p t) d -> p t d", t=PACK)
            nc.sync.dma_start(out=dst[:, ts, cols], in_=y[g, h][:, ts, cols])

        def group_y(g, h, cols, copy):
            if cols.start == 0:
                y_grouped[g, h] = stage.tile(
                    [P, SPAN, PACK], BF16, name="y_grouped", tag="y_grouped", align_bytes=64, bufs=2
                )
            interleave(copy, y_grouped[g, h][:, cols, :], y[g, h][:, :, cols])

        def quantize_y(g, h, cols):
            features = slice(h * SPAN + cols.start, h * SPAN + cols.stop)
            quantize(y_codes[g][:, features], y_scales[4 * g :, features], y_grouped[g, h][:, cols, :])
            dst = out_1[g].rearrange("p d t -> p (d t)").bitcast(I32)
            nc.sync.dma_start(out=dst[:, features], in_=y_codes[g][:, features].bitcast(I32))


        load_tables()
        make_identity(nc, ident[:])
        load_x(0, slice(0, THIRD))
        load_x(0, slice(THIRD, K))
        for s in range(1, X_TILES - 1):
            load_x(s)

        turn_tables()
        spread_tables()
        make_bias_all()
        for i in range(STRIPS * TURNS):
            s, jj = divmod(i, TURNS)
            if i == TURNS:
                for n in range(2):
                    load_x(X_TILES - 1 + n)
                    load_w(n)
            if i == 2 * TURNS:
                load_x(STRIPS - 1)
                for n in range(2, PASSES):
                    load_w(n)
            if i == 1:
                make_row_sum()
            if jj == 0 and 1 <= s <= PACK:
                make_pos(s - 1)
            if i == W0_TURN:
                group_w(0)
            if i == W1_TURN:
                group_w(1)
            if i == FIRST_PRODUCT_TURN:
                multiply_pass(0, 0, 0)
            turn_x(i, PACK if i >= FIRST_PRODUCT_TURN - PACK else 0)
            if i == W0_TURN + 1:
                quantize_w(0)
            if i == W1_TURN + 1:
                quantize_w(1)
            if i % 2 == 0 and i > 0:
                quantize_x(i // 2 - 1)


        group_w(2)
        quantize_x(STRIPS * TURNS // 2 - 1)
        load_w(PASSES)
        for n in range(2, CHUNKS_BEFORE_ADDS):
            if n < PASSES:
                load_w(PASSES + n - 1)
            if n == PASSES - 1:
                load_w(CHUNKS - 1)
            group_w(n + 1)
            quantize_w(n)
        multiply_pass(0, 0, 1)
        multiply_pass(1, 0, 0)
        multiply_pass(1, 0, 1)
        for j in range(2, PASS_MAJOR[0]):
            for g in range(2):
                multiply_pass(g, 0, j)
        for g in range(2):
            for t in range(PACK):
                finish_bank(g, 0, t)
        for t in range(PACK):
            add_bank(0, 0, t)
        store_y(0, 0, slice(0, PACK), whole)
        for n in range(CHUNKS_BEFORE_ADDS, CHUNKS - 1):
            group_w(n + 1)
            quantize_w(n)
        for t in range(PACK):
            add_bank(1, 0, t)
            if t == 0:
                quantize_w(CHUNKS - 1)
        store_y(1, 0, slice(0, PACK), whole)


        group_y(0, 0, whole, nc.scalar.copy)
        group_y(1, 0, whole, nc.scalar.copy)
        for j in range(PASS_MAJOR[1]):
            multiply_pass(0, 1, j)
        for t in range(PACK):
            finish_bank(0, 1, t)
            add_bank(0, 1, t)
            store_y(0, 1, slice(t, t + 1), whole)
            if t == 1:
                quantize_y(0, 0, whole)
        quantize_y(1, 0, whole)
        group_y(0, 1, whole, nc.scalar.copy)


        pairs = [slice(0, 2), slice(2, 4)]
        sums = [multiply_last_unit(ts, front, PACK + i) for i, ts in enumerate(pairs)]
        for ts, part in zip(pairs, sums):
            add_pos(1, 1, ts, front, part[:])
        store_y(1, 1, slice(0, PACK), front)
        group_y(1, 1, front, nc.scalar.copy)
        quantize_y(0, 1, whole)

        for t in range(PACK):
            one = slice(t, t + 1)
            add_pos(1, 1, one, back, multiply_last_unit(one, back, (PACK + 2 + t) % BANKS)[:])
            if t == 2:
                quantize_y(1, 1, front)
            if t % 2 == 1:
                store_y(1, 1, slice(t - 1, t + 1), back)
        cut = HALF + VECTOR_COLS_LAST
        group_y(1, 1, slice(HALF, cut), nc.vector.tensor_copy)
        group_y(1, 1, slice(cut, SPAN), nc.scalar.copy)
        quantize_y(1, 1, back)
        scale_rows = out_2.bitcast(I32)
        for quad in range(4):
            queue = nc.sync if quad % 2 == 0 else nc.scalar
            queue.dma_start(
                out=scale_rows[:, 4 * quad : 4 * quad + 4, :],
                in_=y_scales[32 * quad : 32 * quad + 8, :].bitcast(I32),
            )
